import numpy as np
import ml_dtypes


def mxq(x, axis, fmt="e4m3"):
    dtype, down = {"e4m3": (ml_dtypes.float8_e4m3fn, 7), "e5m2": (ml_dtypes.float8_e5m2, 14)}[fmt]
    v = np.moveaxis(np.asarray(x, np.float32).astype(ml_dtypes.bfloat16).astype(np.float64), axis, -1)
    blocks = v.reshape(v.shape[:-1] + (-1, 32))
    amax = np.abs(blocks).max(-1, keepdims=True)
    byte = np.maximum(np.where(amax > 0, np.frexp(amax)[1] - 1 + 127, 0) - down, 1)
    scale = np.exp2(byte - 127.0)
    codes = (blocks / scale).astype(np.float32).astype(dtype).astype(np.float64)
    return np.moveaxis((codes * scale).reshape(v.shape), -1, axis)


WIDE = False


def mx_kscale(k):
    if not WIDE:
        return np.ones(k)
    levels = np.array([10, -10, 5, -5, 0])
    if k % 512:
        return np.exp2(np.random.permutation(np.resize(levels, k // 32))).repeat(32)
    a = np.empty((k // 512, 16))
    for p in range(k // 512):
        a[p, :8] = np.random.permutation(np.resize(levels, 8))
        for g in range(8):
            far = levels[np.abs(levels - a[p, g]) >= 10]
            a[p, g + 8] = far[np.random.randint(len(far))]
    return np.exp2(a.ravel()).repeat(32)


def f64(x):
    return np.asarray(x).astype(np.float64)


def striped(idx):
    return np.tile(idx.reshape(-1, 16).T, (8, 1)).astype(np.uint16)


def unstriped(offs):
    return offs[:16].T.reshape(-1).astype(np.int64)


E2M1 = np.array([0.0, 0.5, 1.0, 1.5, 2.0, 3.0, 4.0, 6.0, -0.0, -0.5, -1.0, -1.5, -2.0, -3.0, -4.0, -6.0])


def pack_weight(w, fmt):
    k, n = w.shape
    w = f64(np.asarray(w, np.float32).astype(ml_dtypes.bfloat16)).reshape(k // 32, 32, n)
    amax = np.abs(w).max(1)
    if fmt == "e4m3":
        byte = np.frexp(amax)[1] - 1 + 127 - 7
    else:
        mant, ex = np.frexp(amax / 6.0)
        byte = np.where(mant > 0.5, ex, ex - 1) + 127
    byte = np.clip(np.where(amax > 0, byte, 1), 1, 254)
    scaled = (w * np.exp2(127.0 - byte)[:, None, :]).reshape(k, n).astype(np.float32)
    by_word = np.ascontiguousarray(scaled.reshape(k // 512, 128, 4, n).transpose(0, 1, 3, 2))
    if fmt == "e4m3":
        words = by_word.astype(ml_dtypes.float8_e4m3fn).view(np.uint8)
    else:
        c = by_word.astype(ml_dtypes.float4_e2m1fn).view(np.uint8) & 0xF
        words = (c[..., 0::2] | (c[..., 1::2] << 4)).reshape(k // 512, 128, 2 * n)
    return np.ascontiguousarray(words), np.ascontiguousarray(byte.astype(np.uint8).reshape(k // 512, 16, n))


def unpack_weight(words, scales, fmt):
    g, _, n = scales.shape
    words = np.ascontiguousarray(words).reshape(g, 128, n, -1)
    if fmt == "e4m3":
        vals = words.view(ml_dtypes.float8_e4m3fn).astype(np.float64)
    else:
        nib = np.empty((g, 128, n, 4), np.uint8)
        nib[..., 0::2] = words & 0xF
        nib[..., 1::2] = words >> 4
        vals = E2M1[nib]
    vals = vals * np.repeat(np.exp2(scales.astype(np.float64) - 127.0), 8, axis=1)[..., None]
    return vals.transpose(0, 1, 3, 2).reshape(g * 512, n)


def gelu(v):
    return 0.5 * v * (1.0 + np.tanh(np.sqrt(2.0 / np.pi) * (v + 0.044715 * v**3)))


K, K2, T, TB, S, P, H, N = 1024, 512, 4096, 2048, 1024, 512, 1024, 512

def setup_inputs():
    n = np.random.standard_normal
    s = mx_kscale(K)[:, None]
    s2 = mx_kscale(K2)[:, None]
    u = mx_kscale(H)[:, None]
    d = {}
    d["tab_words"], d["tab_scales"] = pack_weight(n((K, T)) * s, "e4m3")
    d["offs"] = striped(np.random.permutation(T)[:S])
    d["tab2_words"], d["tab2_scales"] = pack_weight(n((K2, TB)) * s2, "e4m3")
    d["offs2"] = striped(np.random.permutation(TB)[:P])
    d["pos1"] = striped(np.random.permutation(S)[:P])
    d["w1"] = (n((K, H)) / K**0.5 / s * u.T).astype(np.float32)
    d["w2_words"], d["w2_scales"] = pack_weight(1.3 * n((K, H)) / K**0.5 / s * u.T, "e2m1")
    d["w3"] = (0.8 * n((K2, H)) / K2**0.5 / s2 * u.T).astype(np.float32)
    d["gm"] = (0.6 * n((H, P)) * u).astype(np.float32)
    d["wgs"] = np.exp(0.3 * n((128, P))).astype(np.float32)
    d["fv"] = (2.5 * np.exp(0.3 * n(H)) / u[:, 0]).astype(np.float32)
    d["w4_words"], d["w4_scales"] = pack_weight(n((H, N)) / H**0.5 / u, "e4m3")
    return d

def reference(tab_words, tab_scales, offs, tab2_words, tab2_scales, offs2, pos1, w1, w2_words, w2_scales, w3, gm, wgs, fv, w4_words, w4_scales):
    v = unpack_weight(tab_words, tab_scales, "e4m3")[:, unstriped(offs)]
    v2 = unpack_weight(tab2_words, tab2_scales, "e4m3")[:, unstriped(offs2)]
    w2 = unpack_weight(w2_words, w2_scales, "e2m1")
    w4 = unpack_weight(w4_words, w4_scales, "e4m3")
    lean = mxq(f64(w1), 0, "e4m3").T @ v
    off_centre = w2.T @ v
    a = lean + np.abs(off_centre)
    b = (mxq(f64(w3), 0, "e4m3").T @ v2) + f64(gm)
    placed = np.zeros((H, S))
    placed[:, unstriped(pos1)] = np.tile(f64(wgs), (H // 128, 1)) * b
    z = a / (1.0 + np.exp(-(f64(fv)[:, None] * placed))) - placed
    return w4.T @ mxq(z, 0, "e4m3")

@@ -1,0 +1,372 @@
+from contextlib import ExitStack
+
+import concourse.mybir as mybir
+from concourse.masks import make_identity
+
+F32 = mybir.dt.float32
+BF16 = mybir.dt.bfloat16
+I32 = mybir.dt.int32
+U32 = mybir.dt.uint32
+U16 = mybir.dt.uint16
+U8 = mybir.dt.uint8
+E4M3X4 = mybir.dt.float8_e4m3fn_x4
+E2M1X4 = mybir.dt.float4_e2m1fn_x4
+ALU = mybir.AluOpType
+ACT = mybir.ActivationFunctionType
+
+K, K2, T, TB, S, PL, H, N = 1024, 512, 4096, 2048, 1024, 512, 1024, 512
+FLOPS = 2 * (2 * K * H * S + K2 * H * PL + H * N * S)
+
+P = 128
+PACK = 4
+PASS = P * PACK
+QUADS = 4
+J_TILES = S // P
+
+
+def tile_list_candle_burn_scores_kernel(
+    tc, tab_words, tab_scales, offs, tab2_words, tab2_scales, offs2, pos1,
+    w1, w2_words, w2_scales, w3, gm, wgs, fv, w4_words, w4_scales, out,
+):
+    nc = tc.nc
+    with ExitStack() as ctx:
+        keep = ctx.enter_context(tc.tile_pool(name="keep", bufs=1))
+        ring = ctx.enter_context(tc.tile_pool(name="ring", bufs=1))
+        shared = ctx.enter_context(tc.tile_pool(name="shared", bufs=1))
+        psum = ctx.enter_context(tc.psum_pool(name="psum", bufs=1))
+        banks_taken = []
+
+        def kept(shape, dtype, name):
+            return keep.tile(shape, dtype, name=name, align_bytes=64)
+
+        def shared_tile(shape, dtype, name, place):
+            return shared.tile(shape, dtype, name=name, align_bytes=64, offset=int(place * 8192))
+
+        def next_bank(shape, name):
+            bank = 1 + len(banks_taken) % 7
+            banks_taken.append(bank)
+            return psum.tile(shape, F32, name=name, offset=bank * 2048)
+
+        def first_bank(shape, name):
+            return psum.tile(shape, F32, name=name, offset=0)
+
+        def row_tile(shape, name):
+            return ring.tile(shape, F32, name=name, tag="row", bufs=8, align_bytes=64)
+
+        def words_of(dram):
+            return dram.rearrange("p n i -> p (n i)").bitcast(I32)
+
+        def load_scale_rows(queue, tile, dram, rows_per_quad, pattern):
+            for q in range(QUADS):
+                src = dram[:, 4 * q : 4 * q + 4, :].bitcast(I32)
+                dst = tile[32 * q : 32 * q + rows_per_quad].bitcast(I32)
+                queue.dma_start(dst, src.rearrange(pattern))
+
+        tab2_s = kept([P, 1, TB], U8, "tab2_s")
+        tab_s = kept([P, T // 4], I32, "tab_s")
+        w2_s = kept([P, 2, H], U8, "w2_s")
+        w4_s = kept([P, 2, N], U8, "w4_s")
+        v_s = [kept([P, S], U8, "v_s%d" % g) for g in range(2)]
+        pages = [kept([P, S], F32, "page%d" % i) for i in range(4)]
+        nc.vector.memset(tab2_s[:].bitcast(I32), 0)
+        nc.vector.memset(tab_s[32:64, :], 0)
+        nc.vector.memset(tab_s[64:128, :], 0)
+        nc.vector.memset(pages[0][:], 0.0)
+        nc.gpsimd.memset(pages[1][:], 0.0)
+        for tile in (v_s[0], v_s[1], w2_s, w4_s):
+            nc.gpsimd.memset(tile[:].bitcast(I32), 0)
+
+        offs2_sb = kept([P, PL // 16], U16, "offs2_sb")
+        nc.sync.dma_start(offs2_sb[:], offs2)
+        tab2_w = shared_tile([P, TB], U32, "tab2_w", 0)
+        nc.sync.dma_start(tab2_w[:].bitcast(I32), words_of(tab2_words[0]))
+        load_scale_rows(nc.sync, tab2_s[:], tab2_scales, 4, "a r n -> r a n")
+
+        def load_weight_block(w, k0, a, name, place):
+            raw = shared_tile([P, PACK, PASS], F32, name, place)
+            rows = w[k0 : k0 + PASS, a * PASS : (a + 1) * PASS]
+            nc.sync.dma_start(raw[:], rows.rearrange("(p i) c -> p i c", i=PACK))
+            return raw
+
+        gm_rows = gm.rearrange("(a p t) j -> a t p j", a=2, t=PACK)
+        gm_sb = {}
+
+        def load_gm(s):
+            gm_sb[s] = row_tile([P, PL], "gm%d" % s)
+            nc.sync.dma_start(gm_sb[s][:], gm_rows[s // PACK, s % PACK])
+
+        wgs_rows = wgs.rearrange("(q t) j -> q t j", t=PACK)
+        wgs_first = kept([P, 1, PL], F32, "wgs_first")
+        wgs_rest = kept([P, PACK - 1, PL], F32, "wgs_rest")
+
+        def load_wgs(tile, t0, t1):
+            for q in (0, 2, 1, 3):
+                nc.sync.dma_start(tile[32 * q : 32 * q + 32], wgs_rows[:, t0:t1, :])
+
+        w3_raw = [load_weight_block(w3, 0, 0, "w3_raw0", 10)]
+        nc.sync.dma_start(tab_s[0:32, :], tab_scales.rearrange("a q n -> (a q) n").bitcast(I32))
+        offs_sb = kept([P, S // 16], U16, "offs_sb")
+        nc.sync.dma_start(offs_sb[:], offs)
+        load_wgs(wgs_first, 0, 1)
+        load_gm(0)
+        pos_sb = kept([P, PL // 16], U16, "pos_sb")
+        nc.sync.dma_start(pos_sb[:], pos1)
+        load_gm(1)
+        load_wgs(wgs_rest, 1, PACK)
+        fv_rows = fv.rearrange("(a p t) -> p a t", a=2, t=PACK)
+        fv_early = kept([P, 2], F32, "fv_early")
+        nc.sync.dma_start(fv_early[:], fv_rows[:, 0, 0:2])
+        tab_w = [shared_tile([P, T], U32, "tab_w%d" % g, 6 + 2 * g) for g in range(2)]
+        nc.sync.dma_start(tab_w[0][:].bitcast(I32), words_of(tab_words[0]))
+        load_gm(2)
+        w3_raw.append(load_weight_block(w3, 0, 1, "w3_raw1", 11))
+        nc.sync.dma_start(tab_w[1][:].bitcast(I32), words_of(tab_words[1]))
+        load_gm(3)
+        w1_raw = {}
+        for g in range(2):
+            w1_raw[0, g] = load_weight_block(w1, g * PASS, 0, "w1_raw0%d" % g, 2 + g)
+        w2_w = kept([P, 2, 2 * H], U8, "w2_w")
+        nc.sync.dma_start(w2_w[:].bitcast(I32), w2_words.bitcast(I32).rearrange("g p c -> p g c"))
+        load_scale_rows(nc.sync, w2_s[:], w2_scales, 4, "a r n -> r a n")
+        fv_sb = kept([P, 2, PACK], F32, "fv_sb")
+        nc.sync.dma_start(fv_sb[:], fv_rows)
+        w1_raw[1, 0] = load_weight_block(w1, 0, 1, "w1_raw10", 4)
+        load_gm(4)
+        load_gm(5)
+        w1_raw[1, 1] = load_weight_block(w1, PASS, 1, "w1_raw11", 5)
+        load_gm(6)
+        load_gm(7)
+        w4_w = kept([P, 2, N], U32, "w4_w")
+        nc.sync.dma_start(
+            w4_w[:].bitcast(I32),
+            w4_words.rearrange("g p c i -> p g (c i)").bitcast(I32),
+        )
+
+        load_scale_rows(nc.sync, w4_s[:], w4_scales, 4, "a r n -> r a n")
+        for page in pages[2:]:
+            nc.gpsimd.memset(page[:], 0.0)
+        ident = kept([P, P], F32, "ident")
+        make_identity(nc, ident[:])
+
+        v2_w = kept([P, PL], U32, "v2_w")
+        v2_s = kept([P, PL], U8, "v2_s")
+        nc.vector.tensor_copy(v2_w[:], tab2_w[:].indirect(offs2_sb[:]))
+        nc.vector.tensor_copy(v2_s[:], tab2_s[:].rearrange("p a n -> p (a n)").indirect(offs2_sb[:]))
+
+        w3_c = kept([P, 2, PASS], U32, "w3_c")
+        w3_s = kept([P, 2, PASS], U8, "w3_s")
+
+        def quantise_w3(a, first_copy):
+            grouped = ring.tile([P, PACK, P, PACK], BF16, name="g3_%d" % a, tag="grouped", bufs=2, align_bytes=64)
+            src = w3_raw[a][:].rearrange("p i (m u e) -> p u m i e", u=2, e=2)
+            dst = grouped[:].rearrange("p (u e) m i -> p u m i e", u=2)
+            flat = grouped[:].rearrange("p t m i -> p (t m i)")
+            for u, copy in ((0, first_copy), (1, nc.scalar.copy)):
+                copy(dst[:, u], src[:, u])
+            for u in range(2):
+                cols = slice(256 * u, 256 * (u + 1))
+                nc.vector.quantize_mx(
+                    out=w3_c[:, a, cols].bitcast(E4M3X4),
+                    scales=w3_s[:, a, cols],
+                    in_=flat[:, 1024 * u : 1024 * (u + 1)],
+                )
+            for half in range(2):
+                pages.append(shared_tile([P, S], F32, "page%d" % len(pages), 10 + a + 0.5 * half))
+                nc.gpsimd.memset(pages[-1][:], 0.0)
+
+        gate = {}
+        placed = {0: kept([P, PACK, S], F32, "placed0")}
+        booth = {}
+
+        def booth_features(s):
+            a, t = divmod(s, PACK)
+            cols = slice(P * t, P * (t + 1))
+            acc = first_bank([P, PL], "b_acc%d" % s)
+            nc.tensor.matmul_mx(
+                out=acc[:], lhsT=w3_c[:, a, cols].bitcast(E4M3X4), lhsT_scale=w3_s[:, a, cols],
+                rhs=v2_w[:].bitcast(E4M3X4), rhs_scale=v2_s[:], start=True, stop=True,
+            )
+            booth[s] = ring.tile([P, PL], F32, name="booth%d" % s, tag="booth", bufs=3, align_bytes=64)
+            nc.vector.tensor_tensor(booth[s][:], acc[:], gm_sb[s][:], ALU.add)
+
+        def place(s):
+            a, t = divmod(s, PACK)
+            page = pages[s]
+            weight = wgs_first[:, 0, :] if t == 0 else wgs_rest[:, t - 1, :]
+            nc.vector.tensor_tensor(page[:].indirect(pos_sb[:]), booth[s][:], weight, ALU.mult)
+            if s == PACK:
+                placed[1] = shared_tile([P, PACK, S], F32, "placed1", 2)
+            nc.gpsimd.dma_start(placed[a][:, t, :], page[:])
+
+        def open_gate(s):
+            a, t = divmod(s, PACK)
+            if t == 0:
+                gate[a] = shared_tile([P, PACK, S], F32, "gate%d" % a, 4 * a)
+            factor = fv_early[:, t : t + 1] if s < 2 else fv_sb[:, a, t : t + 1]
+            nc.scalar.activation(gate[a][:, t, :], pages[s][:], ACT.Sigmoid, scale=factor)
+
+        v_w = [kept([P, S], U32, "v_w%d" % g) for g in range(2)]
+        v_s_rows = kept([P, S], U8, "v_s_rows")
+
+        def gather_table_scales():
+            nc.vector.tensor_copy(v_s_rows[:], tab_s[:].bitcast(U8).indirect(offs_sb[:]))
+            for g in range(2):
+                for q in range(QUADS):
+                    first = 16 * g + 4 * q
+                    nc.gpsimd.dma_start(
+                        v_s[g][32 * q : 32 * q + 4, :].bitcast(I32),
+                        v_s_rows[first : first + 4, :].bitcast(I32),
+                    )
+
+        def gather_table_words(g):
+            nc.vector.tensor_copy(v_w[g][:], tab_w[g][:].indirect(offs_sb[:]))
+
+        w1_c = kept([P, 2, H], U32, "w1_c")
+        w1_s = kept([P, 2, H], U8, "w1_s")
+
+        def quantise_w1(a, g):
+            grouped = ring.tile([P, PASS, PACK], BF16, name="g1_%d%d" % (a, g), tag="grouped", bufs=2, align_bytes=64)
+            nc.scalar.copy(
+                grouped[:].rearrange("p (c e) i -> p c i e", e=4),
+                w1_raw[a, g][:].rearrange("p i (c e) -> p c i e", e=4),
+            )
+            cols = slice(a * PASS, (a + 1) * PASS)
+            nc.vector.quantize_mx(
+                out=w1_c[:, g, cols].bitcast(E4M3X4), scales=w1_s[:, g, cols],
+                in_=grouped[:].rearrange("p c i -> p (c i)"),
+            )
+
+        z_c = kept([P, 2, S], U32, "z_c")
+        z_s = kept([P, 2, S], U8, "z_s")
+        turned = {}
+        gated = {}
+        z_bf = {}
+
+        def products(n):
+            a, jt = divmod(n, J_TILES)
+            js = slice(P * jt, P * (jt + 1))
+            cols = slice(a * PASS, (a + 1) * PASS)
+            turned[n] = shared_tile([P, 2, PASS], F32, "turned%d" % n, 6 + 0.5 * (len(turned) % 8))
+            stage = turned[n]
+            lean = next_bank([P, PASS], "lean%d" % n)
+            off = next_bank([P, PASS], "off%d" % n)
+            for g in range(2):
+                nc.tensor.matmul_mx(
+                    out=lean[:], lhsT=v_w[g][:, js].bitcast(E4M3X4), lhsT_scale=v_s[g][:, js],
+                    rhs=w1_c[:, g, cols].bitcast(E4M3X4), rhs_scale=w1_s[:, g, cols],
+                    start=(g == 0), stop=(g == 1),
+                )
+            for g in range(2):
+                nc.tensor.matmul_mx(
+                    out=off[:], lhsT=v_w[g][:, js].bitcast(E4M3X4), lhsT_scale=v_s[g][:, js],
+                    rhs=w2_w[:, g, 2 * a * PASS : 2 * (a + 1) * PASS].bitcast(E2M1X4), rhs_scale=w2_s[:, g, cols],
+                    start=(g == 0), stop=(g == 1),
+                )
+            nc.scalar.copy(
+                stage[:, 0, :].rearrange("j (t m) -> j t m", t=PACK),
+                lean[:].rearrange("j (m t) -> j t m", t=PACK),
+            )
+            nc.scalar.activation(
+                stage[:, 1, :].rearrange("j (t m) -> j t m", t=PACK),
+                off[:].rearrange("j (m t) -> j t m", t=PACK),
+                ACT.Abs,
+            )
+
+        def add_and_gate(n):
+            a, jt = divmod(n, J_TILES)
+            js = slice(P * jt, P * (jt + 1))
+            stage = turned[n]
+            feat = next_bank([P, PACK, P], "feat%d" % n)
+            for t in range(PACK):
+                for part in range(2):
+                    nc.tensor.matmul(
+                        feat[:, t, :], stage[:, part, P * t : P * (t + 1)], ident[:],
+                        is_transpose=True, start=(part == 0), stop=(part == 1),
+                    )
+            gated[n] = row_tile([P, PACK, P], "gated%d" % n)
+            nc.vector.tensor_tensor(gated[n][:], feat[:], gate[a][:, :, js], ALU.mult)
+
+        def subtract_placed(n):
+            a, jt = divmod(n, J_TILES)
+            js = slice(P * jt, P * (jt + 1))
+            z_bf[n] = ring.tile([P, P, PACK], BF16, name="z_bf%d" % n, tag="z_bf", bufs=3, align_bytes=64)
+            nc.vector.tensor_tensor(
+                z_bf[n][:].rearrange("p (c e) t -> p c t e", e=4),
+                gated[n][:].rearrange("p t (c e) -> p c t e", e=4),
+                placed[a][:, :, js].rearrange("p t (c e) -> p c t e", e=4),
+                ALU.subtract,
+            )
+
+        def quantise_z(n):
+            a, jt = divmod(n, J_TILES)
+            js = slice(P * jt, P * (jt + 1))
+            nc.vector.quantize_mx(
+                out=z_c[:, a, js].bitcast(E4M3X4), scales=z_s[:, a, js],
+                in_=z_bf[n][:].rearrange("p j t -> p (j t)"),
+            )
+
+        out_rows = out.rearrange("(nt p) j -> p nt j", p=P)
+
+        def scores(jt):
+            js = slice(P * jt, P * (jt + 1))
+            acc = first_bank([P, N // P, P], "o_acc%d" % jt)
+            for nt in range(N // P):
+                ns = slice(P * nt, P * (nt + 1))
+                for a in range(2):
+                    nc.tensor.matmul_mx(
+                        out=acc[:, nt, :], lhsT=w4_w[:, a, ns].bitcast(E4M3X4), lhsT_scale=w4_s[:, a, ns],
+                        rhs=z_c[:, a, js].bitcast(E4M3X4), rhs_scale=z_s[:, a, js],
+                        start=(a == 0), stop=(a == 1),
+                    )
+            result = row_tile([P, N // P, P], "result%d" % jt)
+            nc.scalar.copy(result[:], acc[:])
+            nc.sync.dma_start(out_rows[:, :, js], result[:])
+
+        quantise_w3(0, nc.vector.tensor_copy)
+        gather_table_scales()
+        booth_features(0)
+        place(0)
+        open_gate(0)
+        booth_features(1)
+        place(1)
+        open_gate(1)
+        gather_table_words(0)
+        booth_features(2)
+        place(2)
+        quantise_w3(1, nc.scalar.copy)
+        gather_table_words(1)
+        booth_features(3)
+        place(3)
+        quantise_w1(0, 0)
+        quantise_w1(0, 1)
+        open_gate(2)
+        open_gate(3)
+        booth_features(4)
+        place(4)
+        booth_features(5)
+        place(5)
+
+        order = [0, 1, 2, 3, 4, 8, 5, 9, 6, 10, 7, 11, 12, 13, 14, 15]
+        units = len(order)
+        lead = 5
+        extra = {
+            1: lambda: (quantise_w1(1, 0), booth_features(6), place(6)),
+            2: lambda: (quantise_w1(1, 1), booth_features(7), place(7)),
+            5: lambda: open_gate(4),
+            6: lambda: open_gate(5),
+            7: lambda: open_gate(6),
+            8: lambda: open_gate(7),
+        }
+        for step in range(units + lead + 3):
+            if step < units:
+                products(order[step])
+            if 0 <= step - lead < units:
+                add_and_gate(order[step - lead])
+            if 0 <= step - lead - 1 < units:
+                subtract_placed(order[step - lead - 1])
+            if 0 <= step - lead - 2 < units:
+                quantise_z(order[step - lead - 2])
+            if 0 <= step - lead - 3 < units and order[step - lead - 3] >= J_TILES:
+                scores(order[step - lead - 3] - J_TILES)
+            if step in extra:
+                extra[step]()

@@ -34,7 +34,6 @@ def tile_list_candle_burn_scores_kernel(
         ring = ctx.enter_context(tc.tile_pool(name="ring", bufs=1))
         shared = ctx.enter_context(tc.tile_pool(name="shared", bufs=1))
         psum = ctx.enter_context(tc.psum_pool(name="psum", bufs=1))
-        banks_taken = []
 
         def kept(shape, dtype, name):
             return keep.tile(shape, dtype, name=name, align_bytes=64)
@@ -42,13 +41,8 @@ def tile_list_candle_burn_scores_kernel(
         def shared_tile(shape, dtype, name, place):
             return shared.tile(shape, dtype, name=name, align_bytes=64, offset=int(place * 8192))
 
-        def next_bank(shape, name):
-            bank = 1 + len(banks_taken) % 7
-            banks_taken.append(bank)
+        def bank_tile(shape, name, bank):
             return psum.tile(shape, F32, name=name, offset=bank * 2048)
-
-        def first_bank(shape, name):
-            return psum.tile(shape, F32, name=name, offset=0)
 
         def row_tile(shape, name):
             return ring.tile(shape, F32, name=name, tag="row", bufs=8, align_bytes=64)
@@ -130,10 +124,10 @@ def tile_list_candle_burn_scores_kernel(
         load_scale_rows(nc.sync, w2_s[:], w2_scales, 4, "a r n -> r a n")
         fv_sb = kept([P, 2, PACK], F32, "fv_sb")
         nc.sync.dma_start(fv_sb[:], fv_rows)
-        w1_raw[1, 0] = load_weight_block(w1, 0, 1, "w1_raw10", 4)
         load_gm(4)
+        for g in range(2):
+            w1_raw[1, g] = load_weight_block(w1, g * PASS, 1, "w1_raw1%d" % g, 4 + g)
         load_gm(5)
-        w1_raw[1, 1] = load_weight_block(w1, PASS, 1, "w1_raw11", 5)
         load_gm(6)
         load_gm(7)
         w4_w = kept([P, 2, N], U32, "w4_w")
@@ -157,7 +151,7 @@ def tile_list_candle_burn_scores_kernel(
         w3_s = kept([P, 2, PASS], U8, "w3_s")
 
         def quantise_w3(a, first_copy):
-            grouped = ring.tile([P, PACK, P, PACK], BF16, name="g3_%d" % a, tag="grouped", bufs=2, align_bytes=64)
+            grouped = shared_tile([P, PACK, P, PACK], BF16, "g3_%d" % a, 12 + 0.5 * a)
             src = w3_raw[a][:].rearrange("p i (m u e) -> p u m i e", u=2, e=2)
             dst = grouped[:].rearrange("p (u e) m i -> p u m i e", u=2)
             flat = grouped[:].rearrange("p t m i -> p (t m i)")
@@ -177,16 +171,21 @@ def tile_list_candle_burn_scores_kernel(
         gate = {}
         placed = {0: kept([P, PACK, S], F32, "placed0")}
         booth = {}
+        booth_bank = [7, 6, 7, 6, 7, 4, 6, 5]
+        feat_bank = [4, 5, 6, 4, 5, 6, 4, 5, 6, 4, 5, 0, 1, 2, 6, 4]
 
         def booth_features(s):
             a, t = divmod(s, PACK)
             cols = slice(P * t, P * (t + 1))
-            acc = first_bank([P, PL], "b_acc%d" % s)
+            acc = bank_tile([P, PL], "b_acc%d" % s, booth_bank[s])
             nc.tensor.matmul_mx(
                 out=acc[:], lhsT=w3_c[:, a, cols].bitcast(E4M3X4), lhsT_scale=w3_s[:, a, cols],
                 rhs=v2_w[:].bitcast(E4M3X4), rhs_scale=v2_s[:], start=True, stop=True,
             )
-            booth[s] = ring.tile([P, PL], F32, name="booth%d" % s, tag="booth", bufs=3, align_bytes=64)
+            if s == PACK:
+                booth[s] = shared_tile([P, PL], F32, "booth%d" % s, 12.5)
+            else:
+                booth[s] = ring.tile([P, PL], F32, name="booth%d" % s, tag="booth", bufs=2, align_bytes=64)
             nc.vector.tensor_tensor(booth[s][:], acc[:], gm_sb[s][:], ALU.add)
 
         def place(s):
@@ -196,7 +195,10 @@ def tile_list_candle_burn_scores_kernel(
             nc.vector.tensor_tensor(page[:].indirect(pos_sb[:]), booth[s][:], weight, ALU.mult)
             if s == PACK:
                 placed[1] = shared_tile([P, PACK, S], F32, "placed1", 2)
-            nc.gpsimd.dma_start(placed[a][:, t, :], page[:])
+            if s < 2:
+                nc.scalar.copy(placed[a][:, t, :], page[:])
+            else:
+                nc.gpsimd.dma_start(placed[a][:, t, :], page[:])
 
         def open_gate(s):
             a, t = divmod(s, PACK)
@@ -225,7 +227,7 @@ def tile_list_candle_burn_scores_kernel(
         w1_s = kept([P, 2, H], U8, "w1_s")
 
         def quantise_w1(a, g):
-            grouped = ring.tile([P, PASS, PACK], BF16, name="g1_%d%d" % (a, g), tag="grouped", bufs=2, align_bytes=64)
+            grouped = shared_tile([P, PASS, PACK], BF16, "g1_%d%d" % (a, g), 12 + 0.5 * g)
             nc.scalar.copy(
                 grouped[:].rearrange("p (c e) i -> p c i e", e=4),
                 w1_raw[a, g][:].rearrange("p i (c e) -> p c i e", e=4),
@@ -239,6 +241,9 @@ def tile_list_candle_burn_scores_kernel(
         z_c = kept([P, 2, S], U32, "z_c")
         z_s = kept([P, 2, S], U8, "z_s")
         turned = {}
+        free_slots = list(range(8))
+        slot_of = {}
+        feat = {}
         gated = {}
         z_bf = {}
 
@@ -246,10 +251,11 @@ def tile_list_candle_burn_scores_kernel(
             a, jt = divmod(n, J_TILES)
             js = slice(P * jt, P * (jt + 1))
             cols = slice(a * PASS, (a + 1) * PASS)
-            turned[n] = shared_tile([P, 2, PASS], F32, "turned%d" % n, 6 + 0.5 * (len(turned) % 8))
-            stage = turned[n]
-            lean = next_bank([P, PASS], "lean%d" % n)
-            off = next_bank([P, PASS], "off%d" % n)
+            first_bank = 2 * (len(turned) % 2)
+            slot_of[n] = free_slots.pop(0)
+            turned[n] = shared_tile([P, 2, PASS], F32, "turned%d" % n, 6 + 0.5 * slot_of[n])
+            lean = bank_tile([P, PASS], "lean%d" % n, first_bank)
+            off = bank_tile([P, PASS], "off%d" % n, first_bank + 1)
             for g in range(2):
                 nc.tensor.matmul_mx(
                     out=lean[:], lhsT=v_w[g][:, js].bitcast(E4M3X4), lhsT_scale=v_s[g][:, js],
@@ -263,64 +269,74 @@ def tile_list_candle_burn_scores_kernel(
                     start=(g == 0), stop=(g == 1),
                 )
             nc.scalar.copy(
-                stage[:, 0, :].rearrange("j (t m) -> j t m", t=PACK),
+                turned[n][:, 0, :].rearrange("j (t m) -> j t m", t=PACK),
                 lean[:].rearrange("j (m t) -> j t m", t=PACK),
             )
             nc.scalar.activation(
-                stage[:, 1, :].rearrange("j (t m) -> j t m", t=PACK),
+                turned[n][:, 1, :].rearrange("j (t m) -> j t m", t=PACK),
                 off[:].rearrange("j (m t) -> j t m", t=PACK),
                 ACT.Abs,
             )
 
-        def add_and_gate(n):
-            a, jt = divmod(n, J_TILES)
-            js = slice(P * jt, P * (jt + 1))
-            stage = turned[n]
-            feat = next_bank([P, PACK, P], "feat%d" % n)
+        def add_turned(n):
+            feat[n] = bank_tile([P, PACK, P], "feat%d" % n, feat_bank[n])
             for t in range(PACK):
                 for part in range(2):
                     nc.tensor.matmul(
-                        feat[:, t, :], stage[:, part, P * t : P * (t + 1)], ident[:],
+                        feat[n][:, t, :], turned[n][:, part, P * t : P * (t + 1)], ident[:],
                         is_transpose=True, start=(part == 0), stop=(part == 1),
                     )
-            gated[n] = row_tile([P, PACK, P], "gated%d" % n)
-            nc.vector.tensor_tensor(gated[n][:], feat[:], gate[a][:, :, js], ALU.mult)
+            free_slots.append(slot_of[n])
 
-        def subtract_placed(n):
+        def columns(n, count):
             a, jt = divmod(n, J_TILES)
-            js = slice(P * jt, P * (jt + 1))
-            z_bf[n] = ring.tile([P, P, PACK], BF16, name="z_bf%d" % n, tag="z_bf", bufs=3, align_bytes=64)
+            return a, slice(P * jt, P * (jt + count))
+
+        def apply_gate(n, count):
+            gated[n] = ring.tile([P, PACK, count * P], F32, name="gated%d" % n, tag="gated", bufs=2, align_bytes=64)
+            for i in range(count):
+                a, js = columns(n + i, 1)
+                nc.vector.tensor_tensor(
+                    gated[n][:, :, P * i : P * (i + 1)], feat[n + i][:], gate[a][:, :, js], ALU.mult
+                )
+
+        def subtract_placed(n, count):
+            a, js = columns(n, count)
+            z_bf[n] = ring.tile([P, count * P, PACK], BF16, name="z_bf%d" % n, tag="z_bf", bufs=2, align_bytes=64)
             nc.vector.tensor_tensor(
-                z_bf[n][:].rearrange("p (c e) t -> p c t e", e=4),
-                gated[n][:].rearrange("p t (c e) -> p c t e", e=4),
-                placed[a][:, :, js].rearrange("p t (c e) -> p c t e", e=4),
+                z_bf[n][:].rearrange("p (c e) t -> p c t e", e=2),
+                gated[n][:].rearrange("p t (c e) -> p c t e", e=2),
+                placed[a][:, :, js].rearrange("p t (c e) -> p c t e", e=2),
                 ALU.subtract,
             )
 
-        def quantise_z(n):
-            a, jt = divmod(n, J_TILES)
-            js = slice(P * jt, P * (jt + 1))
+        def quantise_z(n, count):
+            a, js = columns(n, count)
             nc.vector.quantize_mx(
                 out=z_c[:, a, js].bitcast(E4M3X4), scales=z_s[:, a, js],
                 in_=z_bf[n][:].rearrange("p j t -> p (j t)"),
             )
 
         out_rows = out.rearrange("(nt p) j -> p nt j", p=P)
+        results = []
 
-        def scores(jt):
-            js = slice(P * jt, P * (jt + 1))
-            acc = first_bank([P, N // P, P], "o_acc%d" % jt)
-            for nt in range(N // P):
-                ns = slice(P * nt, P * (nt + 1))
-                for a in range(2):
-                    nc.tensor.matmul_mx(
-                        out=acc[:, nt, :], lhsT=w4_w[:, a, ns].bitcast(E4M3X4), lhsT_scale=w4_s[:, a, ns],
-                        rhs=z_c[:, a, js].bitcast(E4M3X4), rhs_scale=z_s[:, a, js],
-                        start=(a == 0), stop=(a == 1),
-                    )
-            result = row_tile([P, N // P, P], "result%d" % jt)
-            nc.scalar.copy(result[:], acc[:])
-            nc.sync.dma_start(out_rows[:, :, js], result[:])
+        def scores(n, count):
+            js = columns(n, count)[1]
+            per_bank = PACK // count
+            for nt0 in range(0, N // P, per_bank):
+                name = "%d_%d" % (n, nt0)
+                acc = bank_tile([P, per_bank, count * P], "o_acc" + name, (7, 3)[len(results) % 2])
+                for i in range(per_bank):
+                    ns = slice(P * (nt0 + i), P * (nt0 + i + 1))
+                    for a in range(2):
+                        nc.tensor.matmul_mx(
+                            out=acc[:, i, :], lhsT=w4_w[:, a, ns].bitcast(E4M3X4), lhsT_scale=w4_s[:, a, ns],
+                            rhs=z_c[:, a, js].bitcast(E4M3X4), rhs_scale=z_s[:, a, js],
+                            start=(a == 0), stop=(a == 1),
+                        )
+                results.append(row_tile([P, per_bank, count * P], "result" + name))
+                nc.scalar.copy(results[-1][:], acc[:])
+                nc.sync.dma_start(out_rows[:, nt0 : nt0 + per_bank, js], results[-1][:])
 
         quantise_w3(0, nc.vector.tensor_copy)
         gather_table_scales()
@@ -343,30 +359,40 @@ def tile_list_candle_burn_scores_kernel(
         open_gate(3)
         booth_features(4)
         place(4)
-        booth_features(5)
-        place(5)
+        products(0)
+        products(1)
 
-        order = [0, 1, 2, 3, 4, 8, 5, 9, 6, 10, 7, 11, 12, 13, 14, 15]
-        units = len(order)
-        lead = 5
-        extra = {
-            1: lambda: (quantise_w1(1, 0), booth_features(6), place(6)),
-            2: lambda: (quantise_w1(1, 1), booth_features(7), place(7)),
-            5: lambda: open_gate(4),
-            6: lambda: open_gate(5),
-            7: lambda: open_gate(6),
-            8: lambda: open_gate(7),
-        }
-        for step in range(units + lead + 3):
-            if step < units:
-                products(order[step])
-            if 0 <= step - lead < units:
-                add_and_gate(order[step - lead])
-            if 0 <= step - lead - 1 < units:
-                subtract_placed(order[step - lead - 1])
-            if 0 <= step - lead - 2 < units:
-                quantise_z(order[step - lead - 2])
-            if 0 <= step - lead - 3 < units and order[step - lead - 3] >= J_TILES:
-                scores(order[step - lead - 3] - J_TILES)
-            if step in extra:
-                extra[step]()
+        ahead = [[2, 3], [4, 5, 8, 9], [6, 7, 10, 11, 12], [13, 14, 15]]
+        for pair in range(4):
+            n = 2 * pair
+            add_turned(n)
+            add_turned(n + 1)
+            if pair == 3:
+                add_turned(8)
+                open_gate(7)
+            apply_gate(n, 2)
+            if pair < 3:
+                booth_features(5 + pair)
+            for m in ahead[pair]:
+                products(m)
+            subtract_placed(n, 2)
+            if pair < 3:
+                place(5 + pair)
+            quantise_z(n, 2)
+            if pair == 0:
+                quantise_w1(1, 0)
+                quantise_w1(1, 1)
+            if pair < 3:
+                open_gate(4 + pair)
+
+        chunks = [(8, 2), (10, 2), (12, 2), (14, 1), (15, 1)]
+        for n in range(9, 16):
+            add_turned(n)
+            if n == 9:
+                apply_gate(*chunks[0])
+        for i, chunk in enumerate(chunks):
+            if i + 1 < len(chunks):
+                apply_gate(*chunks[i + 1])
+            subtract_placed(*chunk)
+            quantise_z(*chunk)
+            scores(*chunk)

@@ -66,6 +66,8 @@ def tile_list_candle_burn_scores_kernel(
         nc.vector.memset(tab_s[32:64, :], 0)
         nc.vector.memset(tab_s[64:128, :], 0)
         nc.vector.memset(pages[0][:], 0.0)
+        ident = kept([P, P], F32, "ident")
+        make_identity(nc, ident[:])
         nc.gpsimd.memset(pages[1][:], 0.0)
         for tile in (v_s[0], v_s[1], w2_s, w4_s):
             nc.gpsimd.memset(tile[:].bitcast(I32), 0)
@@ -89,39 +91,31 @@ def tile_list_candle_burn_scores_kernel(
             gm_sb[s] = row_tile([P, PL], "gm%d" % s)
             nc.sync.dma_start(gm_sb[s][:], gm_rows[s // PACK, s % PACK])
 
-        wgs_rows = wgs.rearrange("(q t) j -> q t j", t=PACK)
-        wgs_first = kept([P, 1, PL], F32, "wgs_first")
-        wgs_rest = kept([P, PACK - 1, PL], F32, "wgs_rest")
-
-        def load_wgs(tile, t0, t1):
-            for q in (0, 2, 1, 3):
-                nc.sync.dma_start(tile[32 * q : 32 * q + 32], wgs_rows[:, t0:t1, :])
-
+        wgs_sb = shared_tile([P, PL], F32, "wgs_sb", 14)
+        nc.sync.dma_start(wgs_sb[:], wgs)
         w3_raw = [load_weight_block(w3, 0, 0, "w3_raw0", 10)]
         nc.sync.dma_start(tab_s[0:32, :], tab_scales.rearrange("a q n -> (a q) n").bitcast(I32))
         offs_sb = kept([P, S // 16], U16, "offs_sb")
         nc.sync.dma_start(offs_sb[:], offs)
-        load_wgs(wgs_first, 0, 1)
         load_gm(0)
         pos_sb = kept([P, PL // 16], U16, "pos_sb")
         nc.sync.dma_start(pos_sb[:], pos1)
         load_gm(1)
-        load_wgs(wgs_rest, 1, PACK)
         fv_rows = fv.rearrange("(a p t) -> p a t", a=2, t=PACK)
-        fv_early = kept([P, 2], F32, "fv_early")
-        nc.sync.dma_start(fv_early[:], fv_rows[:, 0, 0:2])
+        fv_early = kept([P, 3], F32, "fv_early")
+        nc.sync.dma_start(fv_early[:], fv_rows[:, 0, 0:3])
         tab_w = [shared_tile([P, T], U32, "tab_w%d" % g, 6 + 2 * g) for g in range(2)]
         nc.sync.dma_start(tab_w[0][:].bitcast(I32), words_of(tab_words[0]))
-        load_gm(2)
         w3_raw.append(load_weight_block(w3, 0, 1, "w3_raw1", 11))
+        load_gm(2)
         nc.sync.dma_start(tab_w[1][:].bitcast(I32), words_of(tab_words[1]))
+        load_scale_rows(nc.sync, w2_s[:], w2_scales, 4, "a r n -> r a n")
         load_gm(3)
         w1_raw = {}
         for g in range(2):
             w1_raw[0, g] = load_weight_block(w1, g * PASS, 0, "w1_raw0%d" % g, 2 + g)
         w2_w = kept([P, 2, 2 * H], U8, "w2_w")
         nc.sync.dma_start(w2_w[:].bitcast(I32), w2_words.bitcast(I32).rearrange("g p c -> p g c"))
-        load_scale_rows(nc.sync, w2_s[:], w2_scales, 4, "a r n -> r a n")
         fv_sb = kept([P, 2, PACK], F32, "fv_sb")
         nc.sync.dma_start(fv_sb[:], fv_rows)
         load_gm(4)
@@ -139,8 +133,19 @@ def tile_list_candle_burn_scores_kernel(
         load_scale_rows(nc.sync, w4_s[:], w4_scales, 4, "a r n -> r a n")
         for page in pages[2:]:
             nc.gpsimd.memset(page[:], 0.0)
-        ident = kept([P, P], F32, "ident")
-        make_identity(nc, ident[:])
+
+        wgs_turned = shared_tile([P, PACK, PL // P, QUADS, 32], F32, "wgs_turned", 13)
+        wgs_dealt = [kept([P, PL], F32, "wgs_dealt%d" % t) for t in range(PACK)]
+        wgs_bank = bank_tile([P, PL // P, P], "wgs_bank", 4)
+        for c in range(PL // P):
+            nc.tensor.transpose(wgs_bank[:, c, :], wgs_sb[:, P * c : P * (c + 1)], ident[:])
+        by_slot = wgs_bank[:].rearrange("j c (m t) -> j t c m", t=PACK)
+        for t in range(PACK):
+            nc.scalar.copy(wgs_turned[:, t], by_slot[:, t].unsqueeze(2).to_broadcast([P, PL // P, QUADS, 32]))
+            dealt = bank_tile([P, PL // P, P], "dealt%d" % t, t)
+            for c in range(PL // P):
+                nc.tensor.transpose(dealt[:, c, :], wgs_turned[:, t, c].rearrange("j q m -> j (q m)"), ident[:])
+            nc.scalar.copy(wgs_dealt[t][:], dealt[:].rearrange("p c j -> p (c j)"))
 
         v2_w = kept([P, PL], U32, "v2_w")
         v2_s = kept([P, PL], U8, "v2_s")
@@ -169,7 +174,7 @@ def tile_list_candle_burn_scores_kernel(
                 nc.gpsimd.memset(pages[-1][:], 0.0)
 
         gate = {}
-        placed = {0: kept([P, PACK, S], F32, "placed0")}
+        placed = {}
         booth = {}
         booth_bank = [7, 6, 7, 6, 7, 4, 6, 5]
         feat_bank = [4, 5, 6, 4, 5, 6, 4, 5, 6, 4, 5, 0, 1, 2, 6, 4]
@@ -191,11 +196,10 @@ def tile_list_candle_burn_scores_kernel(
         def place(s):
             a, t = divmod(s, PACK)
             page = pages[s]
-            weight = wgs_first[:, 0, :] if t == 0 else wgs_rest[:, t - 1, :]
-            nc.vector.tensor_tensor(page[:].indirect(pos_sb[:]), booth[s][:], weight, ALU.mult)
-            if s == PACK:
-                placed[1] = shared_tile([P, PACK, S], F32, "placed1", 2)
-            if s < 2:
+            nc.vector.tensor_tensor(page[:].indirect(pos_sb[:]), booth[s][:], wgs_dealt[t][:], ALU.mult)
+            if t == 0:
+                placed[a] = shared_tile([P, PACK, S], F32, "placed%d" % a, (13, 2)[a])
+            if s < 3:
                 nc.scalar.copy(placed[a][:, t, :], page[:])
             else:
                 nc.gpsimd.dma_start(placed[a][:, t, :], page[:])
@@ -204,7 +208,7 @@ def tile_list_candle_burn_scores_kernel(
             a, t = divmod(s, PACK)
             if t == 0:
                 gate[a] = shared_tile([P, PACK, S], F32, "gate%d" % a, 4 * a)
-            factor = fv_early[:, t : t + 1] if s < 2 else fv_sb[:, a, t : t + 1]
+            factor = fv_early[:, t : t + 1] if s < 3 else fv_sb[:, a, t : t + 1]
             nc.scalar.activation(gate[a][:, t, :], pages[s][:], ACT.Sigmoid, scale=factor)
 
         v_w = [kept([P, S], U32, "v_w%d" % g) for g in range(2)]
@@ -322,7 +326,8 @@ def tile_list_candle_burn_scores_kernel(
 
         def scores(n, count):
             js = columns(n, count)[1]
-            per_bank = PACK // count
+            last = n + count == 2 * J_TILES
+            per_bank = 2 if last else PACK // count
             for nt0 in range(0, N // P, per_bank):
                 name = "%d_%d" % (n, nt0)
                 acc = bank_tile([P, per_bank, count * P], "o_acc" + name, (7, 3)[len(results) % 2])
@@ -335,7 +340,8 @@ def tile_list_candle_burn_scores_kernel(
                             start=(a == 0), stop=(a == 1),
                         )
                 results.append(row_tile([P, per_bank, count * P], "result" + name))
-                nc.scalar.copy(results[-1][:], acc[:])
+                empty = nc.vector.tensor_copy if last and nt0 > 0 else nc.scalar.copy
+                empty(results[-1][:], acc[:])
                 nc.sync.dma_start(out_rows[:, nt0 : nt0 + per_bank, js], results[-1][:])
 
         quantise_w3(0, nc.vector.tensor_copy)

@@ -72,6 +72,9 @@ def tile_list_candle_burn_scores_kernel(
         for tile in (v_s[0], v_s[1], w2_s, w4_s):
             nc.gpsimd.memset(tile[:].bitcast(I32), 0)
 
+        offs_sb = kept([P, S // 16], U16, "offs_sb")
+        nc.sync.dma_start(offs_sb[:], offs)
+        nc.sync.dma_start(tab_s[0:32, :], tab_scales.rearrange("a q n -> (a q) n").bitcast(I32))
         offs2_sb = kept([P, PL // 16], U16, "offs2_sb")
         nc.sync.dma_start(offs2_sb[:], offs2)
         tab2_w = shared_tile([P, TB], U32, "tab2_w", 0)
@@ -94,28 +97,25 @@ def tile_list_candle_burn_scores_kernel(
         wgs_sb = shared_tile([P, PL], F32, "wgs_sb", 14)
         nc.sync.dma_start(wgs_sb[:], wgs)
         w3_raw = [load_weight_block(w3, 0, 0, "w3_raw0", 10)]
-        nc.sync.dma_start(tab_s[0:32, :], tab_scales.rearrange("a q n -> (a q) n").bitcast(I32))
-        offs_sb = kept([P, S // 16], U16, "offs_sb")
-        nc.sync.dma_start(offs_sb[:], offs)
         load_gm(0)
         pos_sb = kept([P, PL // 16], U16, "pos_sb")
         nc.sync.dma_start(pos_sb[:], pos1)
         load_gm(1)
         fv_rows = fv.rearrange("(a p t) -> p a t", a=2, t=PACK)
-        fv_early = kept([P, 3], F32, "fv_early")
-        nc.sync.dma_start(fv_early[:], fv_rows[:, 0, 0:3])
+        fv_early = kept([P, 2], F32, "fv_early")
+        nc.sync.dma_start(fv_early[:], fv_rows[:, 0, 0:2])
         tab_w = [shared_tile([P, T], U32, "tab_w%d" % g, 6 + 2 * g) for g in range(2)]
         nc.sync.dma_start(tab_w[0][:].bitcast(I32), words_of(tab_words[0]))
-        w3_raw.append(load_weight_block(w3, 0, 1, "w3_raw1", 11))
         load_gm(2)
         nc.sync.dma_start(tab_w[1][:].bitcast(I32), words_of(tab_words[1]))
         load_scale_rows(nc.sync, w2_s[:], w2_scales, 4, "a r n -> r a n")
-        load_gm(3)
         w1_raw = {}
         for g in range(2):
             w1_raw[0, g] = load_weight_block(w1, g * PASS, 0, "w1_raw0%d" % g, 2 + g)
+        w3_raw.append(load_weight_block(w3, 0, 1, "w3_raw1", 11))
         w2_w = kept([P, 2, 2 * H], U8, "w2_w")
         nc.sync.dma_start(w2_w[:].bitcast(I32), w2_words.bitcast(I32).rearrange("g p c -> p g c"))
+        load_gm(3)
         fv_sb = kept([P, 2, PACK], F32, "fv_sb")
         nc.sync.dma_start(fv_sb[:], fv_rows)
         load_gm(4)
@@ -147,6 +147,15 @@ def tile_list_candle_burn_scores_kernel(
                 nc.tensor.transpose(dealt[:, c, :], wgs_turned[:, t, c].rearrange("j q m -> j (q m)"), ident[:])
             nc.scalar.copy(wgs_dealt[t][:], dealt[:].rearrange("p c j -> p (c j)"))
 
+        v_s_rows = kept([P, S], U8, "v_s_rows")
+        nc.vector.tensor_copy(v_s_rows[:], tab_s[:].bitcast(U8).indirect(offs_sb[:]))
+        for g in range(2):
+            for q in range(QUADS):
+                first = 16 * g + 4 * q
+                nc.gpsimd.dma_start(
+                    v_s[g][32 * q : 32 * q + 4, :].bitcast(I32),
+                    v_s_rows[first : first + 4, :].bitcast(I32),
+                )
         v2_w = kept([P, PL], U32, "v2_w")
         v2_s = kept([P, PL], U8, "v2_s")
         nc.vector.tensor_copy(v2_w[:], tab2_w[:].indirect(offs2_sb[:]))
@@ -156,7 +165,7 @@ def tile_list_candle_burn_scores_kernel(
         w3_s = kept([P, 2, PASS], U8, "w3_s")
 
         def quantise_w3(a, first_copy):
-            grouped = shared_tile([P, PACK, P, PACK], BF16, "g3_%d" % a, 12 + 0.5 * a)
+            grouped = shared_tile([P, PACK, P, PACK], BF16, "g3_%d" % a, 12)
             src = w3_raw[a][:].rearrange("p i (m u e) -> p u m i e", u=2, e=2)
             dst = grouped[:].rearrange("p (u e) m i -> p u m i e", u=2)
             flat = grouped[:].rearrange("p t m i -> p (t m i)")
@@ -177,7 +186,7 @@ def tile_list_candle_burn_scores_kernel(
         placed = {}
         booth = {}
         booth_bank = [7, 6, 7, 6, 7, 4, 6, 5]
-        feat_bank = [4, 5, 6, 4, 5, 6, 4, 5, 6, 4, 5, 0, 1, 2, 6, 4]
+        feat_bank = [4, 5, 6, 4, 5, 6, 4, 5, 6, 0, 1, 2, 3, 4, 5, 6]
 
         def booth_features(s):
             a, t = divmod(s, PACK)
@@ -187,7 +196,7 @@ def tile_list_candle_burn_scores_kernel(
                 out=acc[:], lhsT=w3_c[:, a, cols].bitcast(E4M3X4), lhsT_scale=w3_s[:, a, cols],
                 rhs=v2_w[:].bitcast(E4M3X4), rhs_scale=v2_s[:], start=True, stop=True,
             )
-            if s == PACK:
+            if s == PACK - 1:
                 booth[s] = shared_tile([P, PL], F32, "booth%d" % s, 12.5)
             else:
                 booth[s] = ring.tile([P, PL], F32, name="booth%d" % s, tag="booth", bufs=2, align_bytes=64)
@@ -199,7 +208,7 @@ def tile_list_candle_burn_scores_kernel(
             nc.vector.tensor_tensor(page[:].indirect(pos_sb[:]), booth[s][:], wgs_dealt[t][:], ALU.mult)
             if t == 0:
                 placed[a] = shared_tile([P, PACK, S], F32, "placed%d" % a, (13, 2)[a])
-            if s < 3:
+            if s < 2:
                 nc.scalar.copy(placed[a][:, t, :], page[:])
             else:
                 nc.gpsimd.dma_start(placed[a][:, t, :], page[:])
@@ -208,21 +217,10 @@ def tile_list_candle_burn_scores_kernel(
             a, t = divmod(s, PACK)
             if t == 0:
                 gate[a] = shared_tile([P, PACK, S], F32, "gate%d" % a, 4 * a)
-            factor = fv_early[:, t : t + 1] if s < 3 else fv_sb[:, a, t : t + 1]
+            factor = fv_early[:, t : t + 1] if s < 2 else fv_sb[:, a, t : t + 1]
             nc.scalar.activation(gate[a][:, t, :], pages[s][:], ACT.Sigmoid, scale=factor)
 
         v_w = [kept([P, S], U32, "v_w%d" % g) for g in range(2)]
-        v_s_rows = kept([P, S], U8, "v_s_rows")
-
-        def gather_table_scales():
-            nc.vector.tensor_copy(v_s_rows[:], tab_s[:].bitcast(U8).indirect(offs_sb[:]))
-            for g in range(2):
-                for q in range(QUADS):
-                    first = 16 * g + 4 * q
-                    nc.gpsimd.dma_start(
-                        v_s[g][32 * q : 32 * q + 4, :].bitcast(I32),
-                        v_s_rows[first : first + 4, :].bitcast(I32),
-                    )
 
         def gather_table_words(g):
             nc.vector.tensor_copy(v_w[g][:], tab_w[g][:].indirect(offs_sb[:]))
@@ -245,7 +243,7 @@ def tile_list_candle_burn_scores_kernel(
         z_c = kept([P, 2, S], U32, "z_c")
         z_s = kept([P, 2, S], U8, "z_s")
         turned = {}
-        free_slots = list(range(8))
+        free_slots = [6 + 0.5 * i for i in range(8)] + [15]
         slot_of = {}
         feat = {}
         gated = {}
@@ -257,7 +255,7 @@ def tile_list_candle_burn_scores_kernel(
             cols = slice(a * PASS, (a + 1) * PASS)
             first_bank = 2 * (len(turned) % 2)
             slot_of[n] = free_slots.pop(0)
-            turned[n] = shared_tile([P, 2, PASS], F32, "turned%d" % n, 6 + 0.5 * slot_of[n])
+            turned[n] = shared_tile([P, 2, PASS], F32, "turned%d" % n, slot_of[n])
             lean = bank_tile([P, PASS], "lean%d" % n, first_bank)
             off = bank_tile([P, PASS], "off%d" % n, first_bank + 1)
             for g in range(2):
@@ -296,8 +294,8 @@ def tile_list_candle_burn_scores_kernel(
             a, jt = divmod(n, J_TILES)
             return a, slice(P * jt, P * (jt + count))
 
-        def apply_gate(n, count):
-            gated[n] = ring.tile([P, PACK, count * P], F32, name="gated%d" % n, tag="gated", bufs=2, align_bytes=64)
+        def apply_gate(n, count, tag="gated_a"):
+            gated[n] = ring.tile([P, PACK, count * P], F32, name="gated%d" % n, tag=tag, align_bytes=64)
             for i in range(count):
                 a, js = columns(n + i, 1)
                 nc.vector.tensor_tensor(
@@ -330,7 +328,7 @@ def tile_list_candle_burn_scores_kernel(
             per_bank = 2 if last else PACK // count
             for nt0 in range(0, N // P, per_bank):
                 name = "%d_%d" % (n, nt0)
-                acc = bank_tile([P, per_bank, count * P], "o_acc" + name, (7, 3)[len(results) % 2])
+                acc = bank_tile([P, per_bank, count * P], "o_acc" + name, (7, 0)[len(results) % 2])
                 for i in range(per_bank):
                     ns = slice(P * (nt0 + i), P * (nt0 + i + 1))
                     for a in range(2):
@@ -345,7 +343,6 @@ def tile_list_candle_burn_scores_kernel(
                 nc.sync.dma_start(out_rows[:, nt0 : nt0 + per_bank, js], results[-1][:])
 
         quantise_w3(0, nc.vector.tensor_copy)
-        gather_table_scales()
         booth_features(0)
         place(0)
         open_gate(0)
@@ -355,50 +352,51 @@ def tile_list_candle_burn_scores_kernel(
         gather_table_words(0)
         booth_features(2)
         place(2)
-        quantise_w3(1, nc.scalar.copy)
         gather_table_words(1)
-        booth_features(3)
-        place(3)
         quantise_w1(0, 0)
         quantise_w1(0, 1)
-        open_gate(2)
-        open_gate(3)
+        booth_features(3)
+        place(3)
+        quantise_w3(1, nc.scalar.copy)
         booth_features(4)
         place(4)
-        products(0)
-        products(1)
+        for n in range(4):
+            products(n)
+        open_gate(2)
+        open_gate(3)
 
-        ahead = [[2, 3], [4, 5, 8, 9], [6, 7, 10, 11, 12], [13, 14, 15]]
-        for pair in range(4):
+        ahead = [[4, 5], [6, 7, 8, 9], [10, 11, 12, 13, 14, 15]]
+        add_turned(0)
+        for pair in range(3):
             n = 2 * pair
-            add_turned(n)
             add_turned(n + 1)
-            if pair == 3:
-                add_turned(8)
-                open_gate(7)
             apply_gate(n, 2)
-            if pair < 3:
-                booth_features(5 + pair)
+            booth_features(5 + pair)
+            add_turned(n + 2)
             for m in ahead[pair]:
                 products(m)
             subtract_placed(n, 2)
-            if pair < 3:
-                place(5 + pair)
+            place(5 + pair)
             quantise_z(n, 2)
             if pair == 0:
                 quantise_w1(1, 0)
                 quantise_w1(1, 1)
-            if pair < 3:
-                open_gate(4 + pair)
-
-        chunks = [(8, 2), (10, 2), (12, 2), (14, 1), (15, 1)]
-        for n in range(9, 16):
+            open_gate(4 + pair)
+        open_gate(7)
+        for n in range(7, 13):
             add_turned(n)
-            if n == 9:
-                apply_gate(*chunks[0])
+
+        chunks = [(6, 2), (8, 2), (10, 2), (12, 2), (14, 1), (15, 1)]
+        tags = ("gated_a", "gated_b")
+        apply_gate(*chunks[0])
+        add_turned(13)
+        add_turned(14)
         for i, chunk in enumerate(chunks):
             if i + 1 < len(chunks):
-                apply_gate(*chunks[i + 1])
+                apply_gate(*chunks[i + 1], tags[(i + 1) % 2])
+            if i == 0:
+                add_turned(15)
             subtract_placed(*chunk)
             quantise_z(*chunk)
-            scores(*chunk)
+            if i > 0:
+                scores(*chunk)

@@ -21,7 +21,36 @@ P = 128
 PACK = 4
 PASS = P * PACK
 QUADS = 4
+SLICES = H // P
 J_TILES = S // P
+UNITS = 2 * J_TILES
+MX_ALIGN = 64
+BANK_BYTES = 2048
+
+AT_GATE = (0, 32)
+AT_W1_RAW = (16, 32)
+AT_PLACED = (104, 16)
+AT_TAB_WORDS = (48, 64)
+AT_NINTH_PRODUCT = 120
+AT_W3_RAW = (80, 88)
+AT_CAST = (96, 100)
+AT_WGS_TURNED, AT_WGS_RAW = 104, 112
+
+GATING_BANKS = (4, 5, 6)
+SPARE_BANK = 7
+
+
+def feature_bank(n):
+    if J_TILES < n <= J_TILES + 4:
+        return n - J_TILES - 1
+    turn = n if n <= J_TILES else n - J_TILES - 5
+    return GATING_BANKS[turn % 3]
+
+
+def booth_bank(s):
+    if s <= PACK:
+        return SPARE_BANK - s % 2
+    return feature_bank(2 * (s - PACK - 1))
 
 
 def tile_list_candle_burn_scores_kernel(
@@ -36,32 +65,31 @@ def tile_list_candle_burn_scores_kernel(
         psum = ctx.enter_context(tc.psum_pool(name="psum", bufs=1))
 
         def kept(shape, dtype, name):
-            return keep.tile(shape, dtype, name=name, align_bytes=64)
+            return keep.tile(shape, dtype, name=name, align_bytes=MX_ALIGN)
 
-        def shared_tile(shape, dtype, name, place):
-            return shared.tile(shape, dtype, name=name, align_bytes=64, offset=int(place * 8192))
+        def shared_tile(shape, dtype, name, kib):
+            return shared.tile(shape, dtype, name=name, align_bytes=MX_ALIGN, offset=kib * 1024)
 
         def bank_tile(shape, name, bank):
-            return psum.tile(shape, F32, name=name, offset=bank * 2048)
+            return psum.tile(shape, F32, name=name, offset=bank * BANK_BYTES)
 
         def row_tile(shape, name):
-            return ring.tile(shape, F32, name=name, tag="row", bufs=8, align_bytes=64)
+            return ring.tile(shape, F32, name=name, tag="row", bufs=SLICES, align_bytes=MX_ALIGN)
 
         def words_of(dram):
             return dram.rearrange("p n i -> p (n i)").bitcast(I32)
 
-        def load_scale_rows(queue, tile, dram, rows_per_quad, pattern):
+        def load_scale_rows(tile, dram):
             for q in range(QUADS):
                 src = dram[:, 4 * q : 4 * q + 4, :].bitcast(I32)
-                dst = tile[32 * q : 32 * q + rows_per_quad].bitcast(I32)
-                queue.dma_start(dst, src.rearrange(pattern))
+                nc.sync.dma_start(tile[32 * q : 32 * q + 4].bitcast(I32), src.rearrange("a r n -> r a n"))
 
         tab2_s = kept([P, 1, TB], U8, "tab2_s")
         tab_s = kept([P, T // 4], I32, "tab_s")
         w2_s = kept([P, 2, H], U8, "w2_s")
         w4_s = kept([P, 2, N], U8, "w4_s")
         v_s = [kept([P, S], U8, "v_s%d" % g) for g in range(2)]
-        pages = [kept([P, S], F32, "page%d" % i) for i in range(4)]
+        pages = [kept([P, S], F32, "page%d" % i) for i in range(PACK)]
         nc.vector.memset(tab2_s[:].bitcast(I32), 0)
         nc.vector.memset(tab_s[32:64, :], 0)
         nc.vector.memset(tab_s[64:128, :], 0)
@@ -77,12 +105,12 @@ def tile_list_candle_burn_scores_kernel(
         nc.sync.dma_start(tab_s[0:32, :], tab_scales.rearrange("a q n -> (a q) n").bitcast(I32))
         offs2_sb = kept([P, PL // 16], U16, "offs2_sb")
         nc.sync.dma_start(offs2_sb[:], offs2)
-        tab2_w = shared_tile([P, TB], U32, "tab2_w", 0)
+        tab2_w = shared_tile([P, TB], U32, "tab2_w", AT_GATE[0])
         nc.sync.dma_start(tab2_w[:].bitcast(I32), words_of(tab2_words[0]))
-        load_scale_rows(nc.sync, tab2_s[:], tab2_scales, 4, "a r n -> r a n")
+        load_scale_rows(tab2_s[:], tab2_scales)
 
-        def load_weight_block(w, k0, a, name, place):
-            raw = shared_tile([P, PACK, PASS], F32, name, place)
+        def load_weight_block(w, k0, a, name, kib):
+            raw = shared_tile([P, PACK, PASS], F32, name, kib)
             rows = w[k0 : k0 + PASS, a * PASS : (a + 1) * PASS]
             nc.sync.dma_start(raw[:], rows.rearrange("(p i) c -> p i c", i=PACK))
             return raw
@@ -94,54 +122,53 @@ def tile_list_candle_burn_scores_kernel(
             gm_sb[s] = row_tile([P, PL], "gm%d" % s)
             nc.sync.dma_start(gm_sb[s][:], gm_rows[s // PACK, s % PACK])
 
-        wgs_sb = shared_tile([P, PL], F32, "wgs_sb", 14)
+        wgs_sb = shared_tile([P, PL], F32, "wgs_sb", AT_WGS_RAW)
         nc.sync.dma_start(wgs_sb[:], wgs)
-        w3_raw = [load_weight_block(w3, 0, 0, "w3_raw0", 10)]
+        w3_raw = [load_weight_block(w3, 0, 0, "w3_raw0", AT_W3_RAW[0])]
         load_gm(0)
         pos_sb = kept([P, PL // 16], U16, "pos_sb")
         nc.sync.dma_start(pos_sb[:], pos1)
         load_gm(1)
+        early_gates = 2
         fv_rows = fv.rearrange("(a p t) -> p a t", a=2, t=PACK)
-        fv_early = kept([P, 2], F32, "fv_early")
-        nc.sync.dma_start(fv_early[:], fv_rows[:, 0, 0:2])
-        tab_w = [shared_tile([P, T], U32, "tab_w%d" % g, 6 + 2 * g) for g in range(2)]
+        fv_early = kept([P, early_gates], F32, "fv_early")
+        nc.sync.dma_start(fv_early[:], fv_rows[:, 0, 0:early_gates])
+        tab_w = [shared_tile([P, T], U32, "tab_w%d" % g, AT_TAB_WORDS[g]) for g in range(2)]
         nc.sync.dma_start(tab_w[0][:].bitcast(I32), words_of(tab_words[0]))
         load_gm(2)
         nc.sync.dma_start(tab_w[1][:].bitcast(I32), words_of(tab_words[1]))
-        load_scale_rows(nc.sync, w2_s[:], w2_scales, 4, "a r n -> r a n")
+        load_scale_rows(w2_s[:], w2_scales)
+        load_gm(3)
         w1_raw = {}
         for g in range(2):
-            w1_raw[0, g] = load_weight_block(w1, g * PASS, 0, "w1_raw0%d" % g, 2 + g)
-        w3_raw.append(load_weight_block(w3, 0, 1, "w3_raw1", 11))
+            w1_raw[0, g] = load_weight_block(w1, g * PASS, 0, "w1_raw0%d" % g, AT_W1_RAW[0] + 8 * g)
+        w3_raw.append(load_weight_block(w3, 0, 1, "w3_raw1", AT_W3_RAW[1]))
         w2_w = kept([P, 2, 2 * H], U8, "w2_w")
         nc.sync.dma_start(w2_w[:].bitcast(I32), w2_words.bitcast(I32).rearrange("g p c -> p g c"))
-        load_gm(3)
         fv_sb = kept([P, 2, PACK], F32, "fv_sb")
         nc.sync.dma_start(fv_sb[:], fv_rows)
         load_gm(4)
         for g in range(2):
-            w1_raw[1, g] = load_weight_block(w1, g * PASS, 1, "w1_raw1%d" % g, 4 + g)
-        load_gm(5)
-        load_gm(6)
-        load_gm(7)
+            w1_raw[1, g] = load_weight_block(w1, g * PASS, 1, "w1_raw1%d" % g, AT_W1_RAW[1] + 8 * g)
+        for s in range(PACK + 1, SLICES):
+            load_gm(s)
         w4_w = kept([P, 2, N], U32, "w4_w")
-        nc.sync.dma_start(
-            w4_w[:].bitcast(I32),
-            w4_words.rearrange("g p c i -> p g (c i)").bitcast(I32),
-        )
-
-        load_scale_rows(nc.sync, w4_s[:], w4_scales, 4, "a r n -> r a n")
+        nc.sync.dma_start(w4_w[:].bitcast(I32), w4_words.rearrange("g p c i -> p g (c i)").bitcast(I32))
+        load_scale_rows(w4_s[:], w4_scales)
         for page in pages[2:]:
             nc.gpsimd.memset(page[:], 0.0)
 
-        wgs_turned = shared_tile([P, PACK, PL // P, QUADS, 32], F32, "wgs_turned", 13)
+        wgs_turned = shared_tile([P, PACK, PL // P, QUADS, 32], F32, "wgs_turned", AT_WGS_TURNED)
         wgs_dealt = [kept([P, PL], F32, "wgs_dealt%d" % t) for t in range(PACK)]
-        wgs_bank = bank_tile([P, PL // P, P], "wgs_bank", 4)
+        wgs_bank = bank_tile([P, PL // P, P], "wgs_bank", GATING_BANKS[0])
         for c in range(PL // P):
             nc.tensor.transpose(wgs_bank[:, c, :], wgs_sb[:, P * c : P * (c + 1)], ident[:])
-        by_slot = wgs_bank[:].rearrange("j c (m t) -> j t c m", t=PACK)
+        rows_by_t = wgs_bank[:].rearrange("j c (m t) -> j t c m", t=PACK)
         for t in range(PACK):
-            nc.scalar.copy(wgs_turned[:, t], by_slot[:, t].unsqueeze(2).to_broadcast([P, PL // P, QUADS, 32]))
+            nc.scalar.copy(
+                wgs_turned[:, t].rearrange("j c q m -> j c m q"),
+                rows_by_t[:, t].unsqueeze(3).to_broadcast([P, PL // P, 32, QUADS]),
+            )
             dealt = bank_tile([P, PL // P, P], "dealt%d" % t, t)
             for c in range(PL // P):
                 nc.tensor.transpose(dealt[:, c, :], wgs_turned[:, t, c].rearrange("j q m -> j (q m)"), ident[:])
@@ -165,41 +192,39 @@ def tile_list_candle_burn_scores_kernel(
         w3_s = kept([P, 2, PASS], U8, "w3_s")
 
         def quantise_w3(a, first_copy):
-            grouped = shared_tile([P, PACK, P, PACK], BF16, "g3_%d" % a, 12)
+            cast = shared_tile([P, PACK, P, PACK], BF16, "w3_cast%d" % a, AT_CAST[0])
             src = w3_raw[a][:].rearrange("p i (m u e) -> p u m i e", u=2, e=2)
-            dst = grouped[:].rearrange("p (u e) m i -> p u m i e", u=2)
-            flat = grouped[:].rearrange("p t m i -> p (t m i)")
+            dst = cast[:].rearrange("p (u e) m i -> p u m i e", u=2)
+            flat = cast[:].rearrange("p t m i -> p (t m i)")
             for u, copy in ((0, first_copy), (1, nc.scalar.copy)):
                 copy(dst[:, u], src[:, u])
             for u in range(2):
-                cols = slice(256 * u, 256 * (u + 1))
+                cols = slice(2 * P * u, 2 * P * (u + 1))
                 nc.vector.quantize_mx(
                     out=w3_c[:, a, cols].bitcast(E4M3X4),
                     scales=w3_s[:, a, cols],
-                    in_=flat[:, 1024 * u : 1024 * (u + 1)],
+                    in_=flat[:, 2 * PASS * u : 2 * PASS * (u + 1)],
                 )
             for half in range(2):
-                pages.append(shared_tile([P, S], F32, "page%d" % len(pages), 10 + a + 0.5 * half))
+                pages.append(shared_tile([P, S], F32, "page%d" % len(pages), AT_W3_RAW[a] + 4 * half))
                 nc.gpsimd.memset(pages[-1][:], 0.0)
 
         gate = {}
         placed = {}
         booth = {}
-        booth_bank = [7, 6, 7, 6, 7, 4, 6, 5]
-        feat_bank = [4, 5, 6, 4, 5, 6, 4, 5, 6, 0, 1, 2, 3, 4, 5, 6]
 
         def booth_features(s):
             a, t = divmod(s, PACK)
             cols = slice(P * t, P * (t + 1))
-            acc = bank_tile([P, PL], "b_acc%d" % s, booth_bank[s])
+            acc = bank_tile([P, PL], "b_acc%d" % s, booth_bank(s))
             nc.tensor.matmul_mx(
                 out=acc[:], lhsT=w3_c[:, a, cols].bitcast(E4M3X4), lhsT_scale=w3_s[:, a, cols],
                 rhs=v2_w[:].bitcast(E4M3X4), rhs_scale=v2_s[:], start=True, stop=True,
             )
             if s == PACK - 1:
-                booth[s] = shared_tile([P, PL], F32, "booth%d" % s, 12.5)
+                booth[s] = shared_tile([P, PL], F32, "booth%d" % s, AT_CAST[1])
             else:
-                booth[s] = ring.tile([P, PL], F32, name="booth%d" % s, tag="booth", bufs=2, align_bytes=64)
+                booth[s] = ring.tile([P, PL], F32, name="booth%d" % s, tag="booth", bufs=2, align_bytes=MX_ALIGN)
             nc.vector.tensor_tensor(booth[s][:], acc[:], gm_sb[s][:], ALU.add)
 
         def place(s):
@@ -207,17 +232,18 @@ def tile_list_candle_burn_scores_kernel(
             page = pages[s]
             nc.vector.tensor_tensor(page[:].indirect(pos_sb[:]), booth[s][:], wgs_dealt[t][:], ALU.mult)
             if t == 0:
-                placed[a] = shared_tile([P, PACK, S], F32, "placed%d" % a, (13, 2)[a])
-            if s < 2:
+                placed[a] = shared_tile([P, PACK, S], F32, "placed%d" % a, AT_PLACED[a])
+            if s < early_gates:
                 nc.scalar.copy(placed[a][:, t, :], page[:])
             else:
-                nc.gpsimd.dma_start(placed[a][:, t, :], page[:])
+                queue = nc.gpsimd if a == 0 else nc.sync
+                queue.dma_start(placed[a][:, t, :], page[:])
 
         def open_gate(s):
             a, t = divmod(s, PACK)
             if t == 0:
-                gate[a] = shared_tile([P, PACK, S], F32, "gate%d" % a, 4 * a)
-            factor = fv_early[:, t : t + 1] if s < 2 else fv_sb[:, a, t : t + 1]
+                gate[a] = shared_tile([P, PACK, S], F32, "gate%d" % a, AT_GATE[a])
+            factor = fv_early[:, t : t + 1] if s < early_gates else fv_sb[:, a, t : t + 1]
             nc.scalar.activation(gate[a][:, t, :], pages[s][:], ACT.Sigmoid, scale=factor)
 
         v_w = [kept([P, S], U32, "v_w%d" % g) for g in range(2)]
@@ -229,22 +255,22 @@ def tile_list_candle_burn_scores_kernel(
         w1_s = kept([P, 2, H], U8, "w1_s")
 
         def quantise_w1(a, g):
-            grouped = shared_tile([P, PASS, PACK], BF16, "g1_%d%d" % (a, g), 12 + 0.5 * g)
+            cast = shared_tile([P, PASS, PACK], BF16, "w1_cast%d%d" % (a, g), AT_CAST[g])
             nc.scalar.copy(
-                grouped[:].rearrange("p (c e) i -> p c i e", e=4),
+                cast[:].rearrange("p (c e) i -> p c i e", e=4),
                 w1_raw[a, g][:].rearrange("p i (c e) -> p c i e", e=4),
             )
             cols = slice(a * PASS, (a + 1) * PASS)
             nc.vector.quantize_mx(
                 out=w1_c[:, g, cols].bitcast(E4M3X4), scales=w1_s[:, g, cols],
-                in_=grouped[:].rearrange("p c i -> p (c i)"),
+                in_=cast[:].rearrange("p c i -> p (c i)"),
             )
 
         z_c = kept([P, 2, S], U32, "z_c")
         z_s = kept([P, 2, S], U8, "z_s")
         turned = {}
-        free_slots = [6 + 0.5 * i for i in range(8)] + [15]
-        slot_of = {}
+        free_places = [AT_TAB_WORDS[0] + 4 * i for i in range(8)] + [AT_NINTH_PRODUCT]
+        place_of = {}
         feat = {}
         gated = {}
         z_bf = {}
@@ -254,8 +280,8 @@ def tile_list_candle_burn_scores_kernel(
             js = slice(P * jt, P * (jt + 1))
             cols = slice(a * PASS, (a + 1) * PASS)
             first_bank = 2 * (len(turned) % 2)
-            slot_of[n] = free_slots.pop(0)
-            turned[n] = shared_tile([P, 2, PASS], F32, "turned%d" % n, slot_of[n])
+            place_of[n] = free_places.pop(0)
+            turned[n] = shared_tile([P, 2, PASS], F32, "turned%d" % n, place_of[n])
             lean = bank_tile([P, PASS], "lean%d" % n, first_bank)
             off = bank_tile([P, PASS], "off%d" % n, first_bank + 1)
             for g in range(2):
@@ -271,31 +297,31 @@ def tile_list_candle_burn_scores_kernel(
                     start=(g == 0), stop=(g == 1),
                 )
             nc.scalar.copy(
-                turned[n][:, 0, :].rearrange("j (t m) -> j t m", t=PACK),
-                lean[:].rearrange("j (m t) -> j t m", t=PACK),
+                turned[n][:, 0, :].rearrange("j (u e m) -> j u m e", u=2, e=2),
+                lean[:].rearrange("j (m u e) -> j u m e", u=2, e=2),
             )
             nc.scalar.activation(
-                turned[n][:, 1, :].rearrange("j (t m) -> j t m", t=PACK),
-                off[:].rearrange("j (m t) -> j t m", t=PACK),
+                turned[n][:, 1, :].rearrange("j (u e m) -> j u m e", u=2, e=2),
+                off[:].rearrange("j (m u e) -> j u m e", u=2, e=2),
                 ACT.Abs,
             )
 
         def add_turned(n):
-            feat[n] = bank_tile([P, PACK, P], "feat%d" % n, feat_bank[n])
+            feat[n] = bank_tile([P, PACK, P], "feat%d" % n, feature_bank(n))
             for t in range(PACK):
                 for part in range(2):
                     nc.tensor.matmul(
                         feat[n][:, t, :], turned[n][:, part, P * t : P * (t + 1)], ident[:],
                         is_transpose=True, start=(part == 0), stop=(part == 1),
                     )
-            free_slots.append(slot_of[n])
+            free_places.append(place_of[n])
 
         def columns(n, count):
             a, jt = divmod(n, J_TILES)
             return a, slice(P * jt, P * (jt + count))
 
-        def apply_gate(n, count, tag="gated_a"):
-            gated[n] = ring.tile([P, PACK, count * P], F32, name="gated%d" % n, tag=tag, align_bytes=64)
+        def apply_gate(n, count, tag):
+            gated[n] = ring.tile([P, PACK, count * P], F32, name="gated%d" % n, tag=tag, align_bytes=MX_ALIGN)
             for i in range(count):
                 a, js = columns(n + i, 1)
                 nc.vector.tensor_tensor(
@@ -304,7 +330,7 @@ def tile_list_candle_burn_scores_kernel(
 
         def subtract_placed(n, count):
             a, js = columns(n, count)
-            z_bf[n] = ring.tile([P, count * P, PACK], BF16, name="z_bf%d" % n, tag="z_bf", bufs=2, align_bytes=64)
+            z_bf[n] = ring.tile([P, count * P, PACK], BF16, name="z_bf%d" % n, tag="z_bf", bufs=2, align_bytes=MX_ALIGN)
             nc.vector.tensor_tensor(
                 z_bf[n][:].rearrange("p (c e) t -> p c t e", e=2),
                 gated[n][:].rearrange("p t (c e) -> p c t e", e=2),
@@ -324,11 +350,11 @@ def tile_list_candle_burn_scores_kernel(
 
         def scores(n, count):
             js = columns(n, count)[1]
-            last = n + count == 2 * J_TILES
+            last = n + count == UNITS
             per_bank = 2 if last else PACK // count
             for nt0 in range(0, N // P, per_bank):
                 name = "%d_%d" % (n, nt0)
-                acc = bank_tile([P, per_bank, count * P], "o_acc" + name, (7, 0)[len(results) % 2])
+                acc = bank_tile([P, per_bank, count * P], "o_acc" + name, (SPARE_BANK, 0)[len(results) % 2])
                 for i in range(per_bank):
                     ns = slice(P * (nt0 + i), P * (nt0 + i + 1))
                     for a in range(2):
@@ -343,12 +369,10 @@ def tile_list_candle_burn_scores_kernel(
                 nc.sync.dma_start(out_rows[:, nt0 : nt0 + per_bank, js], results[-1][:])
 
         quantise_w3(0, nc.vector.tensor_copy)
-        booth_features(0)
-        place(0)
-        open_gate(0)
-        booth_features(1)
-        place(1)
-        open_gate(1)
+        for s in range(early_gates):
+            booth_features(s)
+            place(s)
+            open_gate(s)
         gather_table_words(0)
         booth_features(2)
         place(2)
@@ -360,43 +384,44 @@ def tile_list_candle_burn_scores_kernel(
         quantise_w3(1, nc.scalar.copy)
         booth_features(4)
         place(4)
-        for n in range(4):
+        made = 4
+        for n in range(made):
             products(n)
         open_gate(2)
         open_gate(3)
 
-        ahead = [[4, 5], [6, 7, 8, 9], [10, 11, 12, 13, 14, 15]]
+        gated_tags = ("gated_a", "gated_b")
         add_turned(0)
-        for pair in range(3):
+        for pair in range(SLICES - PACK - 1):
             n = 2 * pair
             add_turned(n + 1)
-            apply_gate(n, 2)
-            booth_features(5 + pair)
+            apply_gate(n, 2, gated_tags[0])
+            booth_features(PACK + 1 + pair)
             add_turned(n + 2)
-            for m in ahead[pair]:
+            for m in range(made, made + 2 * (pair + 1)):
                 products(m)
+            made = made + 2 * (pair + 1)
             subtract_placed(n, 2)
-            place(5 + pair)
+            place(PACK + 1 + pair)
             quantise_z(n, 2)
             if pair == 0:
                 quantise_w1(1, 0)
                 quantise_w1(1, 1)
-            open_gate(4 + pair)
-        open_gate(7)
+            open_gate(PACK + pair)
+        open_gate(SLICES - 1)
+
         for n in range(7, 13):
             add_turned(n)
-
-        chunks = [(6, 2), (8, 2), (10, 2), (12, 2), (14, 1), (15, 1)]
-        tags = ("gated_a", "gated_b")
-        apply_gate(*chunks[0])
+        chunks = [(n, 2) for n in range(6, UNITS - 2, 2)] + [(UNITS - 2, 1), (UNITS - 1, 1)]
+        apply_gate(*chunks[0], gated_tags[0])
         add_turned(13)
         add_turned(14)
         for i, chunk in enumerate(chunks):
             if i + 1 < len(chunks):
-                apply_gate(*chunks[i + 1], tags[(i + 1) % 2])
+                apply_gate(*chunks[i + 1], gated_tags[(i + 1) % 2])
             if i == 0:
                 add_turned(15)
             subtract_placed(*chunk)
             quantise_z(*chunk)
-            if i > 0:
+            if chunk[0] >= J_TILES:
                 scores(*chunk)

from contextlib import ExitStack

import concourse.mybir as mybir
from concourse.masks import make_identity

F32 = mybir.dt.float32
BF16 = mybir.dt.bfloat16
I32 = mybir.dt.int32
U32 = mybir.dt.uint32
U16 = mybir.dt.uint16
U8 = mybir.dt.uint8
E4M3X4 = mybir.dt.float8_e4m3fn_x4
E2M1X4 = mybir.dt.float4_e2m1fn_x4
ALU = mybir.AluOpType
ACT = mybir.ActivationFunctionType

K, K2, T, TB, S, PL, H, N = 1024, 512, 4096, 2048, 1024, 512, 1024, 512
FLOPS = 2 * (2 * K * H * S + K2 * H * PL + H * N * S)

P = 128
PACK = 4
PASS = P * PACK
QUADS = 4
SLICES = H // P
J_TILES = S // P
UNITS = 2 * J_TILES
MX_ALIGN = 64
BANK_BYTES = 2048

AT_GATE = (0, 32)
AT_W1_RAW = (16, 32)
AT_PLACED = (104, 16)
AT_TAB_WORDS = (48, 64)
AT_NINTH_PRODUCT = 120
AT_W3_RAW = (80, 88)
AT_CAST = (96, 100)
AT_WGS_TURNED, AT_WGS_RAW = 104, 112

GATING_BANKS = (4, 5, 6)
SPARE_BANK = 7


def feature_bank(n):
    if J_TILES < n <= J_TILES + 4:
        return n - J_TILES - 1
    turn = n if n <= J_TILES else n - J_TILES - 5
    return GATING_BANKS[turn % 3]


def booth_bank(s):
    if s <= PACK:
        return SPARE_BANK - s % 2
    return feature_bank(2 * (s - PACK - 1))


def tile_list_candle_burn_scores_kernel(
    tc, tab_words, tab_scales, offs, tab2_words, tab2_scales, offs2, pos1,
    w1, w2_words, w2_scales, w3, gm, wgs, fv, w4_words, w4_scales, out,
):
    nc = tc.nc
    with ExitStack() as ctx:
        keep = ctx.enter_context(tc.tile_pool(name="keep", bufs=1))
        ring = ctx.enter_context(tc.tile_pool(name="ring", bufs=1))
        shared = ctx.enter_context(tc.tile_pool(name="shared", bufs=1))
        psum = ctx.enter_context(tc.psum_pool(name="psum", bufs=1))

        def kept(shape, dtype, name):
            return keep.tile(shape, dtype, name=name, align_bytes=MX_ALIGN)

        def shared_tile(shape, dtype, name, kib):
            return shared.tile(shape, dtype, name=name, align_bytes=MX_ALIGN, offset=kib * 1024)

        def bank_tile(shape, name, bank):
            return psum.tile(shape, F32, name=name, offset=bank * BANK_BYTES)

        def row_tile(shape, name):
            return ring.tile(shape, F32, name=name, tag="row", bufs=SLICES, align_bytes=MX_ALIGN)

        def words_of(dram):
            return dram.rearrange("p n i -> p (n i)").bitcast(I32)

        def load_scale_rows(tile, dram):
            for q in range(QUADS):
                src = dram[:, 4 * q : 4 * q + 4, :].bitcast(I32)
                nc.sync.dma_start(tile[32 * q : 32 * q + 4].bitcast(I32), src.rearrange("a r n -> r a n"))

        tab2_s = kept([P, 1, TB], U8, "tab2_s")
        tab_s = kept([P, T // 4], I32, "tab_s")
        w2_s = kept([P, 2, H], U8, "w2_s")
        w4_s = kept([P, 2, N], U8, "w4_s")
        v_s = [kept([P, S], U8, "v_s%d" % g) for g in range(2)]
        pages = [kept([P, S], F32, "page%d" % i) for i in range(PACK)]
        nc.vector.memset(tab2_s[:].bitcast(I32), 0)
        nc.vector.memset(tab_s[32:64, :], 0)
        nc.vector.memset(tab_s[64:128, :], 0)
        nc.vector.memset(pages[0][:], 0.0)
        ident = kept([P, P], F32, "ident")
        make_identity(nc, ident[:])
        nc.gpsimd.memset(pages[1][:], 0.0)
        for tile in (v_s[0], v_s[1], w2_s, w4_s):
            nc.gpsimd.memset(tile[:].bitcast(I32), 0)

        offs_sb = kept([P, S // 16], U16, "offs_sb")
        nc.sync.dma_start(offs_sb[:], offs)
        nc.sync.dma_start(tab_s[0:32, :], tab_scales.rearrange("a q n -> (a q) n").bitcast(I32))
        offs2_sb = kept([P, PL // 16], U16, "offs2_sb")
        nc.sync.dma_start(offs2_sb[:], offs2)
        tab2_w = shared_tile([P, TB], U32, "tab2_w", AT_GATE[0])
        nc.sync.dma_start(tab2_w[:].bitcast(I32), words_of(tab2_words[0]))
        load_scale_rows(tab2_s[:], tab2_scales)

        def load_weight_block(w, k0, a, name, kib):
            raw = shared_tile([P, PACK, PASS], F32, name, kib)
            rows = w[k0 : k0 + PASS, a * PASS : (a + 1) * PASS]
            nc.sync.dma_start(raw[:], rows.rearrange("(p i) c -> p i c", i=PACK))
            return raw

        gm_rows = gm.rearrange("(a p t) j -> a t p j", a=2, t=PACK)
        gm_sb = {}

        def load_gm(s):
            gm_sb[s] = row_tile([P, PL], "gm%d" % s)
            nc.sync.dma_start(gm_sb[s][:], gm_rows[s // PACK, s % PACK])

        wgs_sb = shared_tile([P, PL], F32, "wgs_sb", AT_WGS_RAW)
        nc.sync.dma_start(wgs_sb[:], wgs)
        w3_raw = [load_weight_block(w3, 0, 0, "w3_raw0", AT_W3_RAW[0])]
        load_gm(0)
        pos_sb = kept([P, PL // 16], U16, "pos_sb")
        nc.sync.dma_start(pos_sb[:], pos1)
        load_gm(1)
        early_gates = 2
        fv_rows = fv.rearrange("(a p t) -> p a t", a=2, t=PACK)
        fv_early = kept([P, early_gates], F32, "fv_early")
        nc.sync.dma_start(fv_early[:], fv_rows[:, 0, 0:early_gates])
        tab_w = [shared_tile([P, T], U32, "tab_w%d" % g, AT_TAB_WORDS[g]) for g in range(2)]
        nc.sync.dma_start(tab_w[0][:].bitcast(I32), words_of(tab_words[0]))
        load_gm(2)
        nc.sync.dma_start(tab_w[1][:].bitcast(I32), words_of(tab_words[1]))
        load_scale_rows(w2_s[:], w2_scales)
        load_gm(3)
        w1_raw = {}
        for g in range(2):
            w1_raw[0, g] = load_weight_block(w1, g * PASS, 0, "w1_raw0%d" % g, AT_W1_RAW[0] + 8 * g)
        w3_raw.append(load_weight_block(w3, 0, 1, "w3_raw1", AT_W3_RAW[1]))
        w2_w = kept([P, 2, 2 * H], U8, "w2_w")
        nc.sync.dma_start(w2_w[:].bitcast(I32), w2_words.bitcast(I32).rearrange("g p c -> p g c"))
        fv_sb = kept([P, 2, PACK], F32, "fv_sb")
        nc.sync.dma_start(fv_sb[:], fv_rows)
        load_gm(4)
        for g in range(2):
            w1_raw[1, g] = load_weight_block(w1, g * PASS, 1, "w1_raw1%d" % g, AT_W1_RAW[1] + 8 * g)
        for s in range(PACK + 1, SLICES):
            load_gm(s)
        w4_w = kept([P, 2, N], U32, "w4_w")
        nc.sync.dma_start(w4_w[:].bitcast(I32), w4_words.rearrange("g p c i -> p g (c i)").bitcast(I32))
        load_scale_rows(w4_s[:], w4_scales)
        for page in pages[2:]:
            nc.gpsimd.memset(page[:], 0.0)

        wgs_turned = shared_tile([P, PACK, PL // P, QUADS, 32], F32, "wgs_turned", AT_WGS_TURNED)
        wgs_dealt = [kept([P, PL], F32, "wgs_dealt%d" % t) for t in range(PACK)]
        wgs_bank = bank_tile([P, PL // P, P], "wgs_bank", GATING_BANKS[0])
        for c in range(PL // P):
            nc.tensor.transpose(wgs_bank[:, c, :], wgs_sb[:, P * c : P * (c + 1)], ident[:])
        rows_by_t = wgs_bank[:].rearrange("j c (m t) -> j t c m", t=PACK)
        for t in range(PACK):
            nc.scalar.copy(
                wgs_turned[:, t].rearrange("j c q m -> j c m q"),
                rows_by_t[:, t].unsqueeze(3).to_broadcast([P, PL // P, 32, QUADS]),
            )
            dealt = bank_tile([P, PL // P, P], "dealt%d" % t, t)
            for c in range(PL // P):
                nc.tensor.transpose(dealt[:, c, :], wgs_turned[:, t, c].rearrange("j q m -> j (q m)"), ident[:])
            nc.scalar.copy(wgs_dealt[t][:], dealt[:].rearrange("p c j -> p (c j)"))

        v_s_rows = kept([P, S], U8, "v_s_rows")
        nc.vector.tensor_copy(v_s_rows[:], tab_s[:].bitcast(U8).indirect(offs_sb[:]))
        for g in range(2):
            for q in range(QUADS):
                first = 16 * g + 4 * q
                nc.gpsimd.dma_start(
                    v_s[g][32 * q : 32 * q + 4, :].bitcast(I32),
                    v_s_rows[first : first + 4, :].bitcast(I32),
                )
        v2_w = kept([P, PL], U32, "v2_w")
        v2_s = kept([P, PL], U8, "v2_s")
        nc.vector.tensor_copy(v2_w[:], tab2_w[:].indirect(offs2_sb[:]))
        nc.vector.tensor_copy(v2_s[:], tab2_s[:].rearrange("p a n -> p (a n)").indirect(offs2_sb[:]))

        w3_c = kept([P, 2, PASS], U32, "w3_c")
        w3_s = kept([P, 2, PASS], U8, "w3_s")

        def quantise_w3(a, first_copy):
            cast = shared_tile([P, PACK, P, PACK], BF16, "w3_cast%d" % a, AT_CAST[0])
            src = w3_raw[a][:].rearrange("p i (m u e) -> p u m i e", u=2, e=2)
            dst = cast[:].rearrange("p (u e) m i -> p u m i e", u=2)
            flat = cast[:].rearrange("p t m i -> p (t m i)")
            for u, copy in ((0, first_copy), (1, nc.scalar.copy)):
                copy(dst[:, u], src[:, u])
            for u in range(2):
                cols = slice(2 * P * u, 2 * P * (u + 1))
                nc.vector.quantize_mx(
                    out=w3_c[:, a, cols].bitcast(E4M3X4),
                    scales=w3_s[:, a, cols],
                    in_=flat[:, 2 * PASS * u : 2 * PASS * (u + 1)],
                )
            for half in range(2):
                pages.append(shared_tile([P, S], F32, "page%d" % len(pages), AT_W3_RAW[a] + 4 * half))
                nc.gpsimd.memset(pages[-1][:], 0.0)

        gate = {}
        placed = {}
        booth = {}

        def booth_features(s):
            a, t = divmod(s, PACK)
            cols = slice(P * t, P * (t + 1))
            acc = bank_tile([P, PL], "b_acc%d" % s, booth_bank(s))
            nc.tensor.matmul_mx(
                out=acc[:], lhsT=w3_c[:, a, cols].bitcast(E4M3X4), lhsT_scale=w3_s[:, a, cols],
                rhs=v2_w[:].bitcast(E4M3X4), rhs_scale=v2_s[:], start=True, stop=True,
            )
            if s == PACK - 1:
                booth[s] = shared_tile([P, PL], F32, "booth%d" % s, AT_CAST[1])
            else:
                booth[s] = ring.tile([P, PL], F32, name="booth%d" % s, tag="booth", bufs=2, align_bytes=MX_ALIGN)
            nc.vector.tensor_tensor(booth[s][:], acc[:], gm_sb[s][:], ALU.add)

        def place(s):
            a, t = divmod(s, PACK)
            page = pages[s]
            nc.vector.tensor_tensor(page[:].indirect(pos_sb[:]), booth[s][:], wgs_dealt[t][:], ALU.mult)
            if t == 0:
                placed[a] = shared_tile([P, PACK, S], F32, "placed%d" % a, AT_PLACED[a])
            if s < early_gates:
                nc.scalar.copy(placed[a][:, t, :], page[:])
            else:
                queue = nc.gpsimd if a == 0 else nc.sync
                queue.dma_start(placed[a][:, t, :], page[:])

        def open_gate(s):
            a, t = divmod(s, PACK)
            if t == 0:
                gate[a] = shared_tile([P, PACK, S], F32, "gate%d" % a, AT_GATE[a])
            factor = fv_early[:, t : t + 1] if s < early_gates else fv_sb[:, a, t : t + 1]
            nc.scalar.activation(gate[a][:, t, :], pages[s][:], ACT.Sigmoid, scale=factor)

        v_w = [kept([P, S], U32, "v_w%d" % g) for g in range(2)]

        def gather_table_words(g):
            nc.vector.tensor_copy(v_w[g][:], tab_w[g][:].indirect(offs_sb[:]))

        w1_c = kept([P, 2, H], U32, "w1_c")
        w1_s = kept([P, 2, H], U8, "w1_s")

        def quantise_w1(a, g):
            cast = shared_tile([P, PASS, PACK], BF16, "w1_cast%d%d" % (a, g), AT_CAST[g])
            nc.scalar.copy(
                cast[:].rearrange("p (c e) i -> p c i e", e=4),
                w1_raw[a, g][:].rearrange("p i (c e) -> p c i e", e=4),
            )
            cols = slice(a * PASS, (a + 1) * PASS)
            nc.vector.quantize_mx(
                out=w1_c[:, g, cols].bitcast(E4M3X4), scales=w1_s[:, g, cols],
                in_=cast[:].rearrange("p c i -> p (c i)"),
            )

        z_c = kept([P, 2, S], U32, "z_c")
        z_s = kept([P, 2, S], U8, "z_s")
        turned = {}
        free_places = [AT_TAB_WORDS[0] + 4 * i for i in range(8)] + [AT_NINTH_PRODUCT]
        place_of = {}
        feat = {}
        gated = {}
        z_bf = {}

        def products(n):
            a, jt = divmod(n, J_TILES)
            js = slice(P * jt, P * (jt + 1))
            cols = slice(a * PASS, (a + 1) * PASS)
            first_bank = 2 * (len(turned) % 2)
            place_of[n] = free_places.pop(0)
            turned[n] = shared_tile([P, 2, PASS], F32, "turned%d" % n, place_of[n])
            lean = bank_tile([P, PASS], "lean%d" % n, first_bank)
            off = bank_tile([P, PASS], "off%d" % n, first_bank + 1)
            for g in range(2):
                nc.tensor.matmul_mx(
                    out=lean[:], lhsT=v_w[g][:, js].bitcast(E4M3X4), lhsT_scale=v_s[g][:, js],
                    rhs=w1_c[:, g, cols].bitcast(E4M3X4), rhs_scale=w1_s[:, g, cols],
                    start=(g == 0), stop=(g == 1),
                )
            for g in range(2):
                nc.tensor.matmul_mx(
                    out=off[:], lhsT=v_w[g][:, js].bitcast(E4M3X4), lhsT_scale=v_s[g][:, js],
                    rhs=w2_w[:, g, 2 * a * PASS : 2 * (a + 1) * PASS].bitcast(E2M1X4), rhs_scale=w2_s[:, g, cols],
                    start=(g == 0), stop=(g == 1),
                )
            nc.scalar.copy(
                turned[n][:, 0, :].rearrange("j (u e m) -> j u m e", u=2, e=2),
                lean[:].rearrange("j (m u e) -> j u m e", u=2, e=2),
            )
            nc.scalar.activation(
                turned[n][:, 1, :].rearrange("j (u e m) -> j u m e", u=2, e=2),
                off[:].rearrange("j (m u e) -> j u m e", u=2, e=2),
                ACT.Abs,
            )

        def add_turned(n):
            feat[n] = bank_tile([P, PACK, P], "feat%d" % n, feature_bank(n))
            for t in range(PACK):
                for part in range(2):
                    nc.tensor.matmul(
                        feat[n][:, t, :], turned[n][:, part, P * t : P * (t + 1)], ident[:],
                        is_transpose=True, start=(part == 0), stop=(part == 1),
                    )
            free_places.append(place_of[n])

        def columns(n, count):
            a, jt = divmod(n, J_TILES)
            return a, slice(P * jt, P * (jt + count))

        def apply_gate(n, count, tag):
            gated[n] = ring.tile([P, PACK, count * P], F32, name="gated%d" % n, tag=tag, align_bytes=MX_ALIGN)
            for i in range(count):
                a, js = columns(n + i, 1)
                nc.vector.tensor_tensor(
                    gated[n][:, :, P * i : P * (i + 1)], feat[n + i][:], gate[a][:, :, js], ALU.mult
                )

        def subtract_placed(n, count):
            a, js = columns(n, count)
            z_bf[n] = ring.tile([P, count * P, PACK], BF16, name="z_bf%d" % n, tag="z_bf", bufs=2, align_bytes=MX_ALIGN)
            nc.vector.tensor_tensor(
                z_bf[n][:].rearrange("p (c e) t -> p c t e", e=2),
                gated[n][:].rearrange("p t (c e) -> p c t e", e=2),
                placed[a][:, :, js].rearrange("p t (c e) -> p c t e", e=2),
                ALU.subtract,
            )

        def quantise_z(n, count):
            a, js = columns(n, count)
            nc.vector.quantize_mx(
                out=z_c[:, a, js].bitcast(E4M3X4), scales=z_s[:, a, js],
                in_=z_bf[n][:].rearrange("p j t -> p (j t)"),
            )

        out_rows = out.rearrange("(nt p) j -> p nt j", p=P)
        results = []

        def scores(n, count):
            js = columns(n, count)[1]
            last = n + count == UNITS
            per_bank = 2 if last else PACK // count
            for nt0 in range(0, N // P, per_bank):
                name = "%d_%d" % (n, nt0)
                acc = bank_tile([P, per_bank, count * P], "o_acc" + name, (SPARE_BANK, 0)[len(results) % 2])
                for i in range(per_bank):
                    ns = slice(P * (nt0 + i), P * (nt0 + i + 1))
                    for a in range(2):
                        nc.tensor.matmul_mx(
                            out=acc[:, i, :], lhsT=w4_w[:, a, ns].bitcast(E4M3X4), lhsT_scale=w4_s[:, a, ns],
                            rhs=z_c[:, a, js].bitcast(E4M3X4), rhs_scale=z_s[:, a, js],
                            start=(a == 0), stop=(a == 1),
                        )
                results.append(row_tile([P, per_bank, count * P], "result" + name))
                empty = nc.vector.tensor_copy if last and nt0 > 0 else nc.scalar.copy
                empty(results[-1][:], acc[:])
                nc.sync.dma_start(out_rows[:, nt0 : nt0 + per_bank, js], results[-1][:])

        quantise_w3(0, nc.vector.tensor_copy)
        for s in range(early_gates):
            booth_features(s)
            place(s)
            open_gate(s)
        gather_table_words(0)
        booth_features(2)
        place(2)
        gather_table_words(1)
        quantise_w1(0, 0)
        quantise_w1(0, 1)
        booth_features(3)
        place(3)
        quantise_w3(1, nc.scalar.copy)
        booth_features(4)
        place(4)
        made = 4
        for n in range(made):
            products(n)
        open_gate(2)
        open_gate(3)

        gated_tags = ("gated_a", "gated_b")
        add_turned(0)
        for pair in range(SLICES - PACK - 1):
            n = 2 * pair
            add_turned(n + 1)
            apply_gate(n, 2, gated_tags[0])
            booth_features(PACK + 1 + pair)
            add_turned(n + 2)
            for m in range(made, made + 2 * (pair + 1)):
                products(m)
            made = made + 2 * (pair + 1)
            subtract_placed(n, 2)
            place(PACK + 1 + pair)
            quantise_z(n, 2)
            if pair == 0:
                quantise_w1(1, 0)
                quantise_w1(1, 1)
            open_gate(PACK + pair)
        open_gate(SLICES - 1)

        for n in range(7, 13):
            add_turned(n)
        chunks = [(n, 2) for n in range(6, UNITS - 2, 2)] + [(UNITS - 2, 1), (UNITS - 1, 1)]
        apply_gate(*chunks[0], gated_tags[0])
        add_turned(13)
        add_turned(14)
        for i, chunk in enumerate(chunks):
            if i + 1 < len(chunks):
                apply_gate(*chunks[i + 1], gated_tags[(i + 1) % 2])
            if i == 0:
                add_turned(15)
            subtract_placed(*chunk)
            quantise_z(*chunk)
            if chunk[0] >= J_TILES:
                scores(*chunk)
